import numpy as np
import ml_dtypes


def mxq(x, axis, fmt="e4m3"):
    dtype, down = {"e4m3": (ml_dtypes.float8_e4m3fn, 7), "e5m2": (ml_dtypes.float8_e5m2, 14)}[fmt]
    v = np.moveaxis(np.asarray(x, np.float32).astype(ml_dtypes.bfloat16).astype(np.float64), axis, -1)
    blocks = v.reshape(v.shape[:-1] + (-1, 32))
    amax = np.abs(blocks).max(-1, keepdims=True)
    byte = np.maximum(np.where(amax > 0, np.frexp(amax)[1] - 1 + 127, 0) - down, 1)
    scale = np.exp2(byte - 127.0)
    codes = (blocks / scale).astype(np.float32).astype(dtype).astype(np.float64)
    return np.moveaxis((codes * scale).reshape(v.shape), -1, axis)


WIDE = False


def mx_kscale(k):
    if not WIDE:
        return np.ones(k)
    levels = np.array([10, -10, 5, -5, 0])
    if k % 512:
        return np.exp2(np.random.permutation(np.resize(levels, k // 32))).repeat(32)
    a = np.empty((k // 512, 16))
    for p in range(k // 512):
        a[p, :8] = np.random.permutation(np.resize(levels, 8))
        for g in range(8):
            far = levels[np.abs(levels - a[p, g]) >= 10]
            a[p, g + 8] = far[np.random.randint(len(far))]
    return np.exp2(a.ravel()).repeat(32)


def f64(x):
    return np.asarray(x).astype(np.float64)


def striped(idx):
    return np.tile(idx.reshape(-1, 16).T, (8, 1)).astype(np.uint16)


def unstriped(offs):
    return offs[:16].T.reshape(-1).astype(np.int64)


E2M1 = np.array([0.0, 0.5, 1.0, 1.5, 2.0, 3.0, 4.0, 6.0, -0.0, -0.5, -1.0, -1.5, -2.0, -3.0, -4.0, -6.0])


def pack_weight(w, fmt):
    k, n = w.shape
    w = f64(np.asarray(w, np.float32).astype(ml_dtypes.bfloat16)).reshape(k // 32, 32, n)
    amax = np.abs(w).max(1)
    if fmt == "e4m3":
        byte = np.frexp(amax)[1] - 1 + 127 - 7
    else:
        mant, ex = np.frexp(amax / 6.0)
        byte = np.where(mant > 0.5, ex, ex - 1) + 127
    byte = np.clip(np.where(amax > 0, byte, 1), 1, 254)
    scaled = (w * np.exp2(127.0 - byte)[:, None, :]).reshape(k, n).astype(np.float32)
    by_word = np.ascontiguousarray(scaled.reshape(k // 512, 128, 4, n).transpose(0, 1, 3, 2))
    if fmt == "e4m3":
        words = by_word.astype(ml_dtypes.float8_e4m3fn).view(np.uint8)
    else:
        c = by_word.astype(ml_dtypes.float4_e2m1fn).view(np.uint8) & 0xF
        words = (c[..., 0::2] | (c[..., 1::2] << 4)).reshape(k // 512, 128, 2 * n)
    return np.ascontiguousarray(words), np.ascontiguousarray(byte.astype(np.uint8).reshape(k // 512, 16, n))


def unpack_weight(words, scales, fmt):
    g, _, n = scales.shape
    words = np.ascontiguousarray(words).reshape(g, 128, n, -1)
    if fmt == "e4m3":
        vals = words.view(ml_dtypes.float8_e4m3fn).astype(np.float64)
    else:
        nib = np.empty((g, 128, n, 4), np.uint8)
        nib[..., 0::2] = words & 0xF
        nib[..., 1::2] = words >> 4
        vals = E2M1[nib]
    vals = vals * np.repeat(np.exp2(scales.astype(np.float64) - 127.0), 8, axis=1)[..., None]
    return vals.transpose(0, 1, 3, 2).reshape(g * 512, n)


def gelu(v):
    return 0.5 * v * (1.0 + np.tanh(np.sqrt(2.0 / np.pi) * (v + 0.044715 * v**3)))


K, T, S, H, T2, N = 1024, 2048, 512, 1024, 1024, 512


def setup_inputs():
    n = np.random.standard_normal
    s = mx_kscale(K)[:, None]
    u = mx_kscale(H)[:, None]
    tab_words, tab_scales = pack_weight(n((K, T)) * s, "e4m3")
    tab2_words, tab2_scales = pack_weight(n((K, T)) * s, "e4m3")
    w2_words, w2_scales = pack_weight(2.0 * n((K, H)) / np.sqrt(K) / s * u.T, "e2m1")
    w4_words, w4_scales = pack_weight(n((H, N)) / np.sqrt(H) / u, "e4m3")
    return {
        "tab_words": tab_words, "tab_scales": tab_scales,
        "tab2_words": tab2_words, "tab2_scales": tab2_scales,
        "offs": striped(np.random.permutation(T)[:S]),
        "offs2": striped(np.random.permutation(T)[:S]),
        "offs3": striped(np.random.permutation(T2)[:S]),
        "offs4": striped(np.random.permutation(T2)[:S]),
        "w1": (1.2 * n((K, H)) / np.sqrt(K) / s).astype(np.float32),
        "gain": (np.random.uniform(0.8, 1.8, H) * u[:, 0]).astype(np.float32),
        "w2_words": w2_words, "w2_scales": w2_scales,
        "w3": (0.53 * n((K, H)) / np.sqrt(K) / s).astype(np.float32),
        "wg1": np.exp(0.3 * n((128, S))).astype(np.float32),
        "wg2": np.exp(0.3 * n((128, S))).astype(np.float32),
        "dig": (0.6 * n((H, T2)) * u).astype(np.float32),
        "w4_words": w4_words, "w4_scales": w4_scales,
    }


def reference(tab_words, tab_scales, tab2_words, tab2_scales, offs, offs2, offs3, offs4, w1, gain, w2_words, w2_scales, w3, wg1, wg2, dig, w4_words, w4_scales):
    v = unpack_weight(tab_words, tab_scales, "e4m3")[:, unstriped(offs)]
    v2 = unpack_weight(tab2_words, tab2_scales, "e4m3")[:, unstriped(offs2)]
    h1 = f64(gain)[:, None] * np.tanh(mxq(f64(w1), 0, "e4m3").T @ v)
    wave = np.sin(mxq(f64(w3), 0, "e4m3").T @ v2)
    h2 = (unpack_weight(w2_words, w2_scales, "e2m1").T @ v2) * wave
    pa = np.zeros((H, T2))
    pa[:, unstriped(offs3)] = np.tile(f64(wg1), (H // 128, 1)) * h1
    pb = np.zeros((H, T2))
    pb[:, unstriped(offs4)] = np.tile(f64(wg2), (H // 128, 1)) * h2
    z = np.maximum(pa, pb) + f64(dig)
    y = unpack_weight(w4_words, w4_scales, "e4m3").T @ mxq(z, 0, "e4m3")
    return np.abs(y)

@@ -1,0 +1,388 @@
+import math
+from contextlib import ExitStack
+
+import concourse.mybir as mybir
+from concourse.masks import make_identity
+
+K, T, S, H, T2, N = 1024, 2048, 512, 1024, 1024, 512
+FLOPS = 2 * (3 * K * H * S + H * N * T2)
+
+F32 = mybir.dt.float32
+BF16 = mybir.dt.bfloat16
+I32 = mybir.dt.int32
+U32 = mybir.dt.uint32
+U16 = mybir.dt.uint16
+U8 = mybir.dt.uint8
+E4M3 = mybir.dt.float8_e4m3fn_x4
+E2M1 = mybir.dt.float4_e2m1fn_x4
+ACT = mybir.ActivationFunctionType
+ALU = mybir.AluOpType
+
+P = 128
+PACK = 4
+K_PASS = P * PACK
+PASSES = 2
+SLICES = H // P
+HALF = 512
+QUARTER = 256
+CHUNKS = (128, 128, 256, 256, 256)
+
+
+def tile_list_buried_wall_score_kernel(
+    tc, tab_words, tab_scales, tab2_words, tab2_scales, offs, offs2, offs3, offs4,
+    w1, gain, w2_words, w2_scales, w3, wg1, wg2, dig, w4_words, w4_scales, out,
+):
+    nc = tc.nc
+    with ExitStack() as ctx:
+        keep = ctx.enter_context(tc.tile_pool(name="keep", bufs=1))
+        ring = ctx.enter_context(tc.tile_pool(name="ring", bufs=2))
+        cycle = ctx.enter_context(tc.tile_pool(name="cycle", bufs=1))
+        psum = ctx.enter_context(tc.psum_pool(name="psum", bufs=1))
+        banks = [psum.tile([P, HALF], F32, name="bank%d" % b) for b in range(8)]
+
+        def load_list(src, name):
+            tile = keep.tile([P, S // 16], U16, name=name)
+            nc.sync.dma_start(tile[:], src)
+            return tile
+
+        def load_words(src, width, name):
+            tile = keep.tile([P, width], I32, name=name, align_bytes=64)
+            nc.sync.dma_start(tile[:], src.bitcast(I32))
+            return tile
+
+        def zeroed_plane(shape, name, engine=nc.vector):
+            tile = keep.tile(shape, U8, name=name, align_bytes=64)
+            engine.memset(tile[:].bitcast(I32), 0)
+            return tile
+
+        def load_table_scales(tile, src):
+            for q in range(4):
+                nc.sync.dma_start(
+                    tile[:].bitcast(I32)[32 * q : 32 * q + 8, :],
+                    src[:, 4 * q : 4 * q + 4, :].bitcast(I32),
+                )
+
+        def load_weight_scales(tile, src):
+            for q in range(4):
+                nc.sync.dma_start(
+                    tile[:].bitcast(I32)[32 * q : 32 * q + 4, :, :],
+                    src[:, 4 * q : 4 * q + 4, :].bitcast(I32).rearrange("a r c -> r a c"),
+                )
+
+        def load_weight_chunk(w, c0, width):
+            raws = []
+            for a in range(PASSES):
+                raw = ring.tile([P, PACK, width], F32, name="raw", tag="raw", bufs=12)
+                rows = w[a * K_PASS : (a + 1) * K_PASS, c0 : c0 + width]
+                nc.sync.dma_start(raw[:], rows.rearrange("(p j) c -> p j c", j=PACK))
+                raws.append(raw)
+            return raws
+
+        def round_weight_slice(raws, c):
+            i = max(i for i in range(len(CHUNKS)) if starts[i] <= c * P)
+            c0 = c * P - starts[i]
+            grouped = ring.tile([P, PASSES, P, PACK], BF16, name="w_grouped", tag="w_grouped", bufs=5, align_bytes=64)
+            for a in range(PASSES):
+                nc.scalar.copy(
+                    grouped[:, a].rearrange("p (c i) j -> p c j i", i=4),
+                    raws[i][a][:, :, c0 : c0 + P].rearrange("p j (c i) -> p c j i", i=4),
+                )
+            return grouped
+
+        def quantise_weight_slice(grouped, offset, name):
+            codes = cycle.tile([P, PASSES, P], U32, name=name + "_codes", align_bytes=64, offset=offset)
+            scales = cycle.tile([P, PASSES, P], U8, name=name + "_scales", align_bytes=64, offset=offset + 1024)
+            nc.vector.quantize_mx(
+                out=codes[:].rearrange("p a c -> p (a c)").bitcast(E4M3),
+                scales=scales[:].rearrange("p a c -> p (a c)"),
+                in_=grouped[:].rearrange("p a c j -> p (a c j)"),
+            )
+            return codes, scales, 0
+
+        def first_place(c):
+            return 2048 * (c % 3)
+
+        def second_place(c):
+            return 2048 * (3 + c % 4)
+
+        def gather(window, offsets, dtype, name):
+            picked = keep.tile([P, S], dtype, name=name, align_bytes=64)
+            nc.vector.tensor_copy(picked[:], window.bitcast(dtype).indirect(offsets[:]))
+            return picked
+
+        def product(acc, lhs, lhs_scale, rhs, rhs_scale):
+            for a in range(PASSES):
+                nc.tensor.matmul_mx(
+                    out=acc[:], lhsT=lhs[a], lhsT_scale=lhs_scale[a], rhs=rhs[a], rhs_scale=rhs_scale[a],
+                    start=(a == 0), stop=(a == PASSES - 1),
+                )
+            return acc
+
+        def chip_weight(entry):
+            codes, scales, c0 = entry
+            return (
+                [codes[:, a, c0 : c0 + P].bitcast(E4M3) for a in range(PASSES)],
+                [scales[:, a, c0 : c0 + P] for a in range(PASSES)],
+            )
+
+        h1_bank, x_bank, amp_bank, angle_bank = banks[0], banks[1], banks[2], banks[7]
+        z_banks, back_banks = banks[0:2], banks[3:5]
+        out_banks = [banks[5], banks[6], banks[7], banks[2], banks[3], banks[4], banks[0], banks[1]]
+        tail_banks = back_banks + z_banks
+        starts = [sum(CHUNKS[:i]) for i in range(len(CHUNKS))]
+
+
+        v_plane = zeroed_plane([P, T], "v_plane", nc.gpsimd)
+        v2_plane = zeroed_plane([P, PASSES, T], "v2_plane")
+        idx = load_list(offs, "idx")
+        v_words = [load_words(tab_words[0].rearrange("p t i -> p (t i)"), T, "v_words0")]
+        load_table_scales(v_plane, tab_scales)
+        w1_raw = [load_weight_chunk(w1, starts[0], CHUNKS[0])]
+        v_words.append(load_words(tab_words[1].rearrange("p t i -> p (t i)"), T, "v_words1"))
+        idx2 = load_list(offs2, "idx2")
+        load_weight_scales(v2_plane, tab2_scales)
+        w1_raw.append(load_weight_chunk(w1, starts[1], CHUNKS[1]))
+        idx3 = load_list(offs3, "idx3")
+        idx4 = load_list(offs4, "idx4")
+        gain_rows = keep.tile([P, P], F32, name="gain_rows")
+        nc.gpsimd.memset(gain_rows[:], 0.0)
+        nc.sync.dma_start(gain_rows[0:SLICES, :], gain.rearrange("(c p) -> c p", p=P))
+        wg1_sb = keep.tile([P, S], F32, name="wg1_sb")
+        nc.sync.dma_start(wg1_sb[:], wg1)
+        v2_words = [load_words(tab2_words[0].rearrange("p t i -> p (t i)"), T, "v2_words0")]
+        w3_raw = [load_weight_chunk(w3, starts[i], CHUNKS[i]) for i in range(2)]
+        w1_raw.append(load_weight_chunk(w1, starts[2], CHUNKS[2]))
+        v2_words.append(load_words(tab2_words[1].rearrange("p t i -> p (t i)"), T, "v2_words1"))
+        w2_plane = zeroed_plane([P, PASSES, H], "w2_plane")
+        w2_sb = keep.tile([P, PASSES, 2 * H], U8, name="w2_sb", align_bytes=64)
+        nc.sync.dma_start(w2_sb[:].bitcast(I32), w2_words.bitcast(I32).rearrange("a p c -> p a c"))
+        load_weight_scales(w2_plane, w2_scales)
+        wg2_sb = keep.tile([P, S], F32, name="wg2_sb")
+        nc.sync.dma_start(wg2_sb[:], wg2)
+        w1_raw.append(load_weight_chunk(w1, starts[3], CHUNKS[3]))
+        w3_raw.append(load_weight_chunk(w3, starts[2], CHUNKS[2]))
+
+        def load_dig(c):
+            rows = ring.tile([P, T2], F32, name="dig_rows", tag="dig", bufs=4)
+            nc.sync.dma_start(rows[:], dig[c * P : (c + 1) * P, :])
+            return rows
+
+        dig_sb = [load_dig(0)]
+        w1_raw.append(load_weight_chunk(w1, starts[4], CHUNKS[4]))
+        w3_raw.append(load_weight_chunk(w3, starts[3], CHUNKS[3]))
+        dig_sb.append(load_dig(1))
+        w3_raw.append(load_weight_chunk(w3, starts[4], CHUNKS[4]))
+        dig_sb.extend(load_dig(c) for c in (2, 3))
+        w4_plane = zeroed_plane([P, PASSES, N], "w4_plane")
+        w4_sb = [load_words(w4_words[a].rearrange("p n i -> p (n i)"), N, "w4_sb%d" % a) for a in range(PASSES)]
+        load_weight_scales(w4_plane, w4_scales)
+
+        pages_a = [keep.tile([P, T2], F32, name="page_a%d" % c) for c in range(4)]
+        pages_b = [keep.tile([P, T2], F32, name="page_b%d" % c) for c in range(2)]
+        for page in pages_a + pages_b:
+            nc.gpsimd.memset(page[:], 0.0)
+        ident = keep.tile([P, P], F32, name="ident")
+        make_identity(nc, ident[:])
+
+        v_codes = [gather(v_words[0][:], idx, U32, "v_codes0")]
+        v_scales = gather(v_plane[:], idx, U8, "v_scales")
+        v_codes.append(gather(v_words[1][:], idx, U32, "v_codes1"))
+        v_rhs = [v_codes[a][:].bitcast(E4M3) for a in range(PASSES)]
+        v_rhs_scale = [v_scales[4 * a :, :] for a in range(PASSES)]
+
+        w1_q, w3_q = [], []
+
+        def quantise_w1(c, grouped):
+            w1_q.append(quantise_weight_slice(grouped, first_place(c), "w1_%d" % c))
+
+        def quantise_w3(c, grouped):
+            w3_q.append(quantise_weight_slice(grouped, second_place(c), "w3_%d" % c))
+
+        def place_first(c):
+            product(h1_bank, *chip_weight(w1_q[c]), v_rhs, v_rhs_scale)
+            th = ring.tile([P, S], F32, name="th", tag="th")
+            nc.scalar.activation(th[:], h1_bank[:], ACT.Tanh)
+            nc.vector.tensor_tensor(pages_a[c % 4][:].indirect(idx3[:]), th[:], wg1_sb[:], ALU.mult)
+
+        quantise_w1(0, round_weight_slice(w1_raw, 0))
+        place_first(0)
+        quantise_w1(1, round_weight_slice(w1_raw, 1))
+        v2_scales = [gather(v2_plane[:, a, :], idx2, U8, "v2_scales%d" % a) for a in range(PASSES)]
+
+        v2_codes = [gather(v2_words[a][:], idx2, U32, "v2_codes%d" % a) for a in range(PASSES)]
+        v2_rhs = [v2_codes[a][:].bitcast(E4M3) for a in range(PASSES)]
+        v2_rhs_scale = [v2_scales[a][:] for a in range(PASSES)]
+
+        def reduce_angle(c):
+            codes, scales, c0 = w3_q[c]
+            for j0 in range(0, S, P):
+                for a in range(PASSES):
+                    nc.tensor.matmul_mx(
+                        out=x_bank[:, j0 : j0 + P],
+                        lhsT=v2_codes[a][:, j0 : j0 + P].bitcast(E4M3), lhsT_scale=v2_scales[a][:, j0 : j0 + P],
+                        rhs=codes[:, a, :].bitcast(E4M3), rhs_scale=scales[:, a, :],
+                        start=(a == 0), stop=(a == PASSES - 1),
+                    )
+            y = ring.tile([P, S], F32, name="y", tag="y")
+            nc.scalar.activation(y[:], x_bank[:], ACT.Abs, bias=-math.pi / 2)
+            turns = ring.tile([P, S], U32, name="turns", tag="turns")
+            nc.scalar.activation(turns[:], y[:], ACT.Copy, scale=1 / (2 * math.pi))
+            back = ring.tile([P, S], F32, name="back", tag="back")
+            nc.scalar.activation(back[:], turns[:], ACT.Copy, scale=-2 * math.pi)
+            return y, back
+
+        def wave(c, y, back):
+            for k, term in enumerate((y, back)):
+                for j0 in range(0, S, P):
+                    nc.tensor.matmul(
+                        angle_bank[:, j0 : j0 + P], term[:, j0 : j0 + P], ident[:],
+                        start=(k == 0 and j0 == 0), stop=(k == 1 and j0 == S - P), is_transpose=True,
+                    )
+            angle = cycle.tile([P, S], F32, name="angle%d" % c, offset=first_place(c + 5))
+            nc.scalar.activation(angle[:], angle_bank[:], ACT.Abs)
+            nc.scalar.activation(angle[:], angle[:], ACT.Sin, scale=-1.0, bias=math.pi / 2)
+            return angle
+
+        def place_second(c, angle):
+            product(
+                amp_bank,
+                [w2_sb[:, a, 2 * P * c : 2 * P * (c + 1)].bitcast(E2M1) for a in range(PASSES)],
+                [w2_plane[:, a, P * c : P * (c + 1)] for a in range(PASSES)],
+                v2_rhs, v2_rhs_scale,
+            )
+            amp = cycle.tile([P, S], F32, name="amp%d" % c, offset=second_place(c))
+            nc.vector.tensor_tensor(amp[:], amp_bank[:], wg2_sb[:], ALU.mult)
+            page_b = pages_b[c % 2]
+            nc.vector.tensor_tensor(page_b[:].indirect(idx4[:]), angle[:], amp[:], ALU.mult)
+            parts = []
+            width = QUARTER if c == SLICES - 1 else HALF
+            for m0 in range(0, T2, width):
+                cols = slice(m0, m0 + width)
+                larger = ring.tile([P, width], F32, name="larger", tag="larger", bufs=4)
+                nc.vector.scalar_tensor_tensor(
+                    larger[:], pages_a[c % 4][:, cols], gain_sb[:, c : c + 1], page_b[:, cols], ALU.mult, ALU.max
+                )
+                parts.append(larger)
+            return parts
+
+        def turn_dig(c, part, blocks, bank):
+            m0 = part * blocks * P
+            for i in range(blocks):
+                nc.tensor.matmul(
+                    bank[:, i * P : (i + 1) * P], dig_sb[c][:, m0 + i * P : m0 + (i + 1) * P],
+                    ident[:], start=(i == 0), stop=False, is_transpose=True,
+                )
+
+        def add_larger(c, part, larger, bank, copy):
+            blocks = larger.shape[1] // P
+            for i in range(blocks):
+                nc.tensor.matmul(
+                    bank[:, i * P : (i + 1) * P], larger[:, i * P : (i + 1) * P],
+                    ident[:], start=False, stop=(i == blocks - 1), is_transpose=True,
+                )
+            q0 = 32 * (c % 4)
+            h, i0 = divmod(part * blocks, 4)
+            copy(
+                z_t[c // 4][h][:, i0 : i0 + blocks, :, q0 : q0 + 32, :],
+                bank[:, 0 : blocks * P].rearrange("p (i q u e) -> p i u q e", i=blocks, u=2, e=2),
+            )
+
+        def turn_back(z_half, g, back, copy):
+            words = z_half[:].rearrange("p i u q e -> p (i u q e)").bitcast(F32)
+            for i in range(4):
+                col = (4 * g + i) * P
+                nc.tensor.transpose(back[:, i * P : (i + 1) * P], words[:, col : col + P], ident[:])
+            grouped = ring.tile([P, QUARTER, PACK], BF16, name="z_grouped", tag="w_grouped", bufs=5, align_bytes=64)
+            copy(
+                grouped[:].rearrange("p m j -> p (m j)").bitcast(F32).rearrange("p (i m u) -> p i m u", i=2, u=2),
+                back[:].rearrange("p (i u m) -> p i m u", i=2, u=2),
+            )
+            return grouped
+
+        def quantise_z(grouped, name, place):
+            if place is None:
+                codes = keep.tile([P, QUARTER], U32, name=name + "_codes", align_bytes=64)
+            else:
+                codes = cycle.tile([P, QUARTER], U32, name=name + "_codes", align_bytes=64, offset=place)
+            scales = keep.tile([P, QUARTER], U8, name=name + "_scales", align_bytes=64)
+            nc.vector.quantize_mx(out=codes[:].bitcast(E4M3), scales=scales[:], in_=grouped[:].rearrange("p m j -> p (m j)"))
+            return codes, scales
+
+        place_first(1)
+        quantise_w3(0, round_weight_slice(w3_raw, 0))
+        quantise_w3(1, round_weight_slice(w3_raw, 1))
+        quantise_w1(2, round_weight_slice(w1_raw, 2))
+        quantise_w1(3, round_weight_slice(w1_raw, 3))
+        place_first(2)
+        staged = [reduce_angle(0), reduce_angle(1)]
+        angles = [wave(0, *staged[0])]
+        nc.tensor.transpose(banks[6][:, 0:P], gain_rows[:], ident[:])
+        gain_sb = keep.tile([P, SLICES], F32, name="gain_sb")
+        nc.scalar.copy(gain_sb[:], banks[6][:, 0:SLICES])
+        quantise_w1(4, round_weight_slice(w1_raw, 4))
+        quantise_w3(2, round_weight_slice(w3_raw, 2))
+        quantise_w3(3, round_weight_slice(w3_raw, 3))
+
+        z_q = [[], []]
+        z_t = [[keep.tile([P, 4, 2, P, 2], BF16, name="z_t%d_%d" % (b, h)) for h in range(2)] for b in range(PASSES)]
+        placed = []
+        for c in range(SLICES):
+            if c + 3 < SLICES:
+                place_first(c + 3)
+            if c + 2 < SLICES:
+                staged.append(reduce_angle(c + 2))
+            if c + 1 < SLICES:
+                angles.append(wave(c + 1, *staged[c + 1]))
+            if c >= 1:
+                for h in range(2):
+                    turn_dig(c - 1, h, 4, z_banks[h])
+                    add_larger(c - 1, h, placed[c - 1][h], z_banks[h], nc.scalar.copy)
+                if c + 3 < SLICES:
+                    dig_sb.append(load_dig(c + 3))
+            if c + 5 < SLICES:
+                w1_next = round_weight_slice(w1_raw, c + 5)
+            if c + 4 < SLICES:
+                w3_next = round_weight_slice(w3_raw, c + 4)
+            placed.append(place_second(c, angles[c]))
+            if c + 5 < SLICES:
+                quantise_w1(c + 5, w1_next)
+            if c + 4 < SLICES:
+                quantise_w3(c + 4, w3_next)
+            if c in (4, 5):
+                for g in range(2):
+                    grouped = turn_back(z_t[0][c - 4], g, back_banks[g], nc.scalar.copy)
+                    z_q[0].append(quantise_z(grouped, "z0_%d_%d" % (c - 4, g), second_place(c) + 1024 * g))
+
+        def score_pass(a, quarter, pair):
+            acc = out_banks[2 * quarter + pair]
+            codes, scales = z_q[a][quarter]
+            for j in range(2):
+                n0 = (2 * pair + j) * P
+                nc.tensor.matmul_mx(
+                    out=acc[:, j * QUARTER : (j + 1) * QUARTER],
+                    lhsT=w4_sb[a][:, n0 : n0 + P].bitcast(E4M3), lhsT_scale=w4_plane[:, a, n0 : n0 + P],
+                    rhs=codes[:].bitcast(E4M3), rhs_scale=scales[:],
+                    start=(a == 0 and j == 0), stop=(a == PASSES - 1 and j == 1),
+                )
+
+        for quarter in range(2):
+            for pair in range(2):
+                score_pass(0, quarter, pair)
+        for quarter in range(4):
+            turn_dig(SLICES - 1, quarter, 2, tail_banks[quarter])
+        for quarter in range(4):
+            add_larger(SLICES - 1, quarter, placed[-1][quarter], tail_banks[quarter], (nc.scalar.copy, nc.vector.tensor_copy)[quarter // 2])
+        for quarter in range(4):
+            h, g = divmod(quarter, 2)
+            grouped = turn_back(z_t[1][h], g, tail_banks[quarter], (nc.scalar.copy, nc.vector.tensor_copy)[h])
+            z_q[1].append(quantise_z(grouped, "z1_%d" % quarter, None))
+        for quarter in range(4):
+            for pair in range(2):
+                acc = out_banks[2 * quarter + pair]
+                if quarter >= 2:
+                    score_pass(0, quarter, pair)
+                score_pass(1, quarter, pair)
+                score = ring.tile([P, HALF], F32, name="score", tag=("score", "larger")[quarter // 2], bufs=4)
+                nc.scalar.activation(score[:], acc[:], ACT.Abs)
+                rows = out[2 * pair * P : 2 * (pair + 1) * P, quarter * QUARTER : (quarter + 1) * QUARTER]
+                nc.sync.dma_start(rows.rearrange("(j p) m -> p j m", p=P), score[:].rearrange("p (j m) -> p j m", j=2))

@@ -131,6 +131,9 @@ def tile_list_buried_wall_score_kernel(
         tail_banks = back_banks + z_banks
         starts = [sum(CHUNKS[:i]) for i in range(len(CHUNKS))]
 
+        table = keep.tile([P, 1], F32, name="table")
+        nc.vector.memset(table[:], 0.0)
+        nc.scalar.activation(table[:], table[:], ACT.Silu)
 
         v_plane = zeroed_plane([P, T], "v_plane", nc.gpsimd)
         v2_plane = zeroed_plane([P, PASSES, T], "v2_plane")

@@ -25,7 +25,7 @@ PASSES = 2
 SLICES = H // P
 HALF = 512
 QUARTER = 256
-CHUNKS = (128, 128, 256, 256, 256)
+CHUNKS = (256, 256, 256, 256)
 
 
 def tile_list_buried_wall_score_kernel(
@@ -125,7 +125,8 @@ def tile_list_buried_wall_score_kernel(
                 [scales[:, a, c0 : c0 + P] for a in range(PASSES)],
             )
 
-        h1_bank, x_bank, amp_bank, angle_bank = banks[0], banks[1], banks[2], banks[7]
+        h1_bank, x_bank = banks[0], banks[1]
+        amp_banks, angle_banks = (banks[5], banks[2]), (banks[6], banks[7])
         z_banks, back_banks = banks[0:2], banks[3:5]
         out_banks = [banks[5], banks[6], banks[7], banks[2], banks[3], banks[4], banks[0], banks[1]]
         tail_banks = back_banks + z_banks
@@ -136,25 +137,25 @@ def tile_list_buried_wall_score_kernel(
         nc.scalar.activation(table[:], table[:], ACT.Silu)
 
         v_plane = zeroed_plane([P, T], "v_plane", nc.gpsimd)
-        v2_plane = zeroed_plane([P, PASSES, T], "v2_plane")
+        v2_plane = zeroed_plane([P, T], "v2_plane")
+        v2_second = zeroed_plane([P, S], "v2_second")
         idx = load_list(offs, "idx")
         v_words = [load_words(tab_words[0].rearrange("p t i -> p (t i)"), T, "v_words0")]
         load_table_scales(v_plane, tab_scales)
         w1_raw = [load_weight_chunk(w1, starts[0], CHUNKS[0])]
         v_words.append(load_words(tab_words[1].rearrange("p t i -> p (t i)"), T, "v_words1"))
         idx2 = load_list(offs2, "idx2")
-        load_weight_scales(v2_plane, tab2_scales)
-        w1_raw.append(load_weight_chunk(w1, starts[1], CHUNKS[1]))
+        load_table_scales(v2_plane, tab2_scales)
         idx3 = load_list(offs3, "idx3")
+        wg1_sb = keep.tile([P, S], F32, name="wg1_sb")
+        nc.sync.dma_start(wg1_sb[:], wg1)
         idx4 = load_list(offs4, "idx4")
         gain_rows = keep.tile([P, P], F32, name="gain_rows")
         nc.gpsimd.memset(gain_rows[:], 0.0)
         nc.sync.dma_start(gain_rows[0:SLICES, :], gain.rearrange("(c p) -> c p", p=P))
-        wg1_sb = keep.tile([P, S], F32, name="wg1_sb")
-        nc.sync.dma_start(wg1_sb[:], wg1)
         v2_words = [load_words(tab2_words[0].rearrange("p t i -> p (t i)"), T, "v2_words0")]
-        w3_raw = [load_weight_chunk(w3, starts[i], CHUNKS[i]) for i in range(2)]
-        w1_raw.append(load_weight_chunk(w1, starts[2], CHUNKS[2]))
+        w3_raw = [load_weight_chunk(w3, starts[0], CHUNKS[0])]
+        w1_raw.append(load_weight_chunk(w1, starts[1], CHUNKS[1]))
         v2_words.append(load_words(tab2_words[1].rearrange("p t i -> p (t i)"), T, "v2_words1"))
         w2_plane = zeroed_plane([P, PASSES, H], "w2_plane")
         w2_sb = keep.tile([P, PASSES, 2 * H], U8, name="w2_sb", align_bytes=64)
@@ -162,8 +163,8 @@ def tile_list_buried_wall_score_kernel(
         load_weight_scales(w2_plane, w2_scales)
         wg2_sb = keep.tile([P, S], F32, name="wg2_sb")
         nc.sync.dma_start(wg2_sb[:], wg2)
-        w1_raw.append(load_weight_chunk(w1, starts[3], CHUNKS[3]))
-        w3_raw.append(load_weight_chunk(w3, starts[2], CHUNKS[2]))
+        w1_raw.append(load_weight_chunk(w1, starts[2], CHUNKS[2]))
+        w3_raw.append(load_weight_chunk(w3, starts[1], CHUNKS[1]))
 
         def load_dig(c):
             rows = ring.tile([P, T2], F32, name="dig_rows", tag="dig", bufs=4)
@@ -171,19 +172,21 @@ def tile_list_buried_wall_score_kernel(
             return rows
 
         dig_sb = [load_dig(0)]
-        w1_raw.append(load_weight_chunk(w1, starts[4], CHUNKS[4]))
-        w3_raw.append(load_weight_chunk(w3, starts[3], CHUNKS[3]))
+        w1_raw.append(load_weight_chunk(w1, starts[3], CHUNKS[3]))
+        w3_raw.append(load_weight_chunk(w3, starts[2], CHUNKS[2]))
         dig_sb.append(load_dig(1))
-        w3_raw.append(load_weight_chunk(w3, starts[4], CHUNKS[4]))
+        w3_raw.append(load_weight_chunk(w3, starts[3], CHUNKS[3]))
         dig_sb.extend(load_dig(c) for c in (2, 3))
         w4_plane = zeroed_plane([P, PASSES, N], "w4_plane")
         w4_sb = [load_words(w4_words[a].rearrange("p n i -> p (n i)"), N, "w4_sb%d" % a) for a in range(PASSES)]
         load_weight_scales(w4_plane, w4_scales)
 
         pages_a = [keep.tile([P, T2], F32, name="page_a%d" % c) for c in range(4)]
-        pages_b = [keep.tile([P, T2], F32, name="page_b%d" % c) for c in range(2)]
-        for page in pages_a + pages_b:
+        pages_b = [keep.tile([P, T2], F32, name="page_b%d" % c) for c in range(1)]
+        for page in pages_a[:3]:
             nc.gpsimd.memset(page[:], 0.0)
+        for page in pages_a[3:] + pages_b:
+            nc.vector.memset(page[:], 0.0)
         ident = keep.tile([P, P], F32, name="ident")
         make_identity(nc, ident[:])
 
@@ -208,13 +211,18 @@ def tile_list_buried_wall_score_kernel(
             nc.vector.tensor_tensor(pages_a[c % 4][:].indirect(idx3[:]), th[:], wg1_sb[:], ALU.mult)
 
         quantise_w1(0, round_weight_slice(w1_raw, 0))
-        place_first(0)
         quantise_w1(1, round_weight_slice(w1_raw, 1))
-        v2_scales = [gather(v2_plane[:, a, :], idx2, U8, "v2_scales%d" % a) for a in range(PASSES)]
+        place_first(0)
+        v2_scales = gather(v2_plane[:], idx2, U8, "v2_scales")
+        for q in range(4):
+            nc.gpsimd.dma_start(
+                v2_second[:].bitcast(I32)[32 * q : 32 * q + 4, :],
+                v2_scales[:].bitcast(I32)[32 * q + 4 : 32 * q + 8, :],
+            )
 
         v2_codes = [gather(v2_words[a][:], idx2, U32, "v2_codes%d" % a) for a in range(PASSES)]
         v2_rhs = [v2_codes[a][:].bitcast(E4M3) for a in range(PASSES)]
-        v2_rhs_scale = [v2_scales[a][:] for a in range(PASSES)]
+        v2_rhs_scale = [v2_scales[:], v2_second[:]]
 
         def reduce_angle(c):
             codes, scales, c0 = w3_q[c]
@@ -222,7 +230,7 @@ def tile_list_buried_wall_score_kernel(
                 for a in range(PASSES):
                     nc.tensor.matmul_mx(
                         out=x_bank[:, j0 : j0 + P],
-                        lhsT=v2_codes[a][:, j0 : j0 + P].bitcast(E4M3), lhsT_scale=v2_scales[a][:, j0 : j0 + P],
+                        lhsT=v2_codes[a][:, j0 : j0 + P].bitcast(E4M3), lhsT_scale=v2_scales[4 * a :, j0 : j0 + P],
                         rhs=codes[:, a, :].bitcast(E4M3), rhs_scale=scales[:, a, :],
                         start=(a == 0), stop=(a == PASSES - 1),
                     )
@@ -235,6 +243,7 @@ def tile_list_buried_wall_score_kernel(
             return y, back
 
         def wave(c, y, back):
+            angle_bank = angle_banks[c % 2]
             for k, term in enumerate((y, back)):
                 for j0 in range(0, S, P):
                     nc.tensor.matmul(
@@ -247,6 +256,7 @@ def tile_list_buried_wall_score_kernel(
             return angle
 
         def place_second(c, angle):
+            amp_bank = amp_banks[c % 2]
             product(
                 amp_bank,
                 [w2_sb[:, a, 2 * P * c : 2 * P * (c + 1)].bitcast(E2M1) for a in range(PASSES)],
@@ -255,7 +265,7 @@ def tile_list_buried_wall_score_kernel(
             )
             amp = cycle.tile([P, S], F32, name="amp%d" % c, offset=second_place(c))
             nc.vector.tensor_tensor(amp[:], amp_bank[:], wg2_sb[:], ALU.mult)
-            page_b = pages_b[c % 2]
+            page_b = pages_b[0]
             nc.vector.tensor_tensor(page_b[:].indirect(idx4[:]), angle[:], amp[:], ALU.mult)
             parts = []
             width = QUARTER if c == SLICES - 1 else HALF
@@ -319,9 +329,9 @@ def tile_list_buried_wall_score_kernel(
         place_first(2)
         staged = [reduce_angle(0), reduce_angle(1)]
         angles = [wave(0, *staged[0])]
-        nc.tensor.transpose(banks[6][:, 0:P], gain_rows[:], ident[:])
+        nc.tensor.transpose(banks[3][:, 0:P], gain_rows[:], ident[:])
         gain_sb = keep.tile([P, SLICES], F32, name="gain_sb")
-        nc.scalar.copy(gain_sb[:], banks[6][:, 0:SLICES])
+        nc.scalar.copy(gain_sb[:], banks[3][:, 0:SLICES])
         quantise_w1(4, round_weight_slice(w1_raw, 4))
         quantise_w3(2, round_weight_slice(w3_raw, 2))
         quantise_w3(3, round_weight_slice(w3_raw, 3))

@@ -22,10 +22,22 @@ P = 128
 PACK = 4
 K_PASS = P * PACK
 PASSES = 2
+QUADRANTS = 4
 SLICES = H // P
-HALF = 512
+SLICES_A_PASS = K_PASS // P
+BANK = 512
 QUARTER = 256
-CHUNKS = (256, 256, 256, 256)
+CHUNK = 256
+PLACE = 2048
+
+LEAD_W1, LEAD_FIRST_PAGE = 5, 3
+LEAD_W3, LEAD_TURNS, LEAD_WAVE = 4, 2, 1
+FIRST_PAGES = LEAD_FIRST_PAGE + 1
+W1_PLACES, W3_PLACES = 3, 4
+RAW_BUFS = 12
+GROUPED_BUFS = 5
+DIG_BUFS = 4
+OUT_BUFS = 4
 
 
 def tile_list_buried_wall_score_kernel(
@@ -36,335 +48,206 @@ def tile_list_buried_wall_score_kernel(
     with ExitStack() as ctx:
         keep = ctx.enter_context(tc.tile_pool(name="keep", bufs=1))
         ring = ctx.enter_context(tc.tile_pool(name="ring", bufs=2))
-        cycle = ctx.enter_context(tc.tile_pool(name="cycle", bufs=1))
+        shared = ctx.enter_context(tc.tile_pool(name="shared", bufs=1))
         psum = ctx.enter_context(tc.psum_pool(name="psum", bufs=1))
-        banks = [psum.tile([P, HALF], F32, name="bank%d" % b) for b in range(8)]
+        banks = [psum.tile([P, BANK], F32, name="bank%d" % b) for b in range(8)]
+
+        h1_bank, x_bank = banks[0], banks[1]
+        z_banks, back_banks = banks[0:2], banks[3:5]
+        amp_banks, angle_banks = (banks[5], banks[2]), (banks[6], banks[7])
+        tail_banks = back_banks + z_banks
+        out_banks = [banks[5], banks[6], banks[7], banks[2]] + tail_banks
+
+        def w1_place(c):
+            return PLACE * (c % W1_PLACES)
+
+        def w3_place(c):
+            return PLACE * (W1_PLACES + c % W3_PLACES)
 
         def load_list(src, name):
             tile = keep.tile([P, S // 16], U16, name=name)
             nc.sync.dma_start(tile[:], src)
             return tile
 
-        def load_words(src, width, name):
-            tile = keep.tile([P, width], I32, name=name, align_bytes=64)
-            nc.sync.dma_start(tile[:], src.bitcast(I32))
+        def load_words(src, name):
+            tile = keep.tile([P, src.shape[1]], I32, name=name, align_bytes=64)
+            nc.sync.dma_start(tile[:], src.rearrange("p c t -> p (c t)").bitcast(I32))
             return tile
 
-        def zeroed_plane(shape, name, engine=nc.vector):
+        def load_rows(src, name):
+            tile = keep.tile([P, S], F32, name=name)
+            nc.sync.dma_start(tile[:], src)
+            return tile
+
+        def zeroed_scales(shape, name, engine):
             tile = keep.tile(shape, U8, name=name, align_bytes=64)
             engine.memset(tile[:].bitcast(I32), 0)
             return tile
 
         def load_table_scales(tile, src):
-            for q in range(4):
+            for q in range(QUADRANTS):
                 nc.sync.dma_start(
                     tile[:].bitcast(I32)[32 * q : 32 * q + 8, :],
                     src[:, 4 * q : 4 * q + 4, :].bitcast(I32),
                 )
 
         def load_weight_scales(tile, src):
-            for q in range(4):
+            for q in range(QUADRANTS):
                 nc.sync.dma_start(
                     tile[:].bitcast(I32)[32 * q : 32 * q + 4, :, :],
                     src[:, 4 * q : 4 * q + 4, :].bitcast(I32).rearrange("a r c -> r a c"),
                 )
 
-        def load_weight_chunk(w, c0, width):
+        def load_weight_chunk(w, i):
             raws = []
             for a in range(PASSES):
-                raw = ring.tile([P, PACK, width], F32, name="raw", tag="raw", bufs=12)
-                rows = w[a * K_PASS : (a + 1) * K_PASS, c0 : c0 + width]
-                nc.sync.dma_start(raw[:], rows.rearrange("(p j) c -> p j c", j=PACK))
+                raw = ring.tile([P, PACK, CHUNK], F32, name="raw", tag="raw", bufs=RAW_BUFS)
+                rows = w[a * K_PASS : (a + 1) * K_PASS, i * CHUNK : (i + 1) * CHUNK]
+                nc.sync.dma_start(raw[:], rows.rearrange("(p t) c -> p t c", t=PACK))
                 raws.append(raw)
             return raws
 
-        def round_weight_slice(raws, c):
-            i = max(i for i in range(len(CHUNKS)) if starts[i] <= c * P)
-            c0 = c * P - starts[i]
-            grouped = ring.tile([P, PASSES, P, PACK], BF16, name="w_grouped", tag="w_grouped", bufs=5, align_bytes=64)
+        def load_dig(c):
+            rows = ring.tile([P, T2], F32, name="dig_rows", tag="dig", bufs=DIG_BUFS)
+            nc.sync.dma_start(rows[:], dig[c * P : (c + 1) * P, :])
+            return rows
+
+        def round_weight_slice(chunks, c):
+            i, c0 = divmod(c * P, CHUNK)
+            grouped = ring.tile([P, PASSES, P, PACK], BF16, name="w_grouped", tag="grouped", bufs=GROUPED_BUFS, align_bytes=64)
             for a in range(PASSES):
-                nc.scalar.copy(
-                    grouped[:, a].rearrange("p (c i) j -> p c j i", i=4),
-                    raws[i][a][:, :, c0 : c0 + P].rearrange("p j (c i) -> p c j i", i=4),
-                )
+                nc.scalar.copy(grouped[:, a], chunks[i][a][:, :, c0 : c0 + P].rearrange("p t c -> p c t"))
             return grouped
 
-        def quantise_weight_slice(grouped, offset, name):
-            codes = cycle.tile([P, PASSES, P], U32, name=name + "_codes", align_bytes=64, offset=offset)
-            scales = cycle.tile([P, PASSES, P], U8, name=name + "_scales", align_bytes=64, offset=offset + 1024)
+        def quantise_weight_slice(grouped, place, name):
+            codes = shared.tile([P, PASSES, P], U32, name=name + "_codes", align_bytes=64, offset=place)
+            scales = shared.tile([P, PASSES, P], U8, name=name + "_scales", align_bytes=64, offset=place + PLACE // 2)
             nc.vector.quantize_mx(
                 out=codes[:].rearrange("p a c -> p (a c)").bitcast(E4M3),
                 scales=scales[:].rearrange("p a c -> p (a c)"),
-                in_=grouped[:].rearrange("p a c j -> p (a c j)"),
+                in_=grouped[:].rearrange("p a c t -> p (a c t)"),
             )
-            return codes, scales, 0
+            return codes, scales
 
-        def first_place(c):
-            return 2048 * (c % 3)
+        def quantise_w1(c, grouped):
+            w1_q.append(quantise_weight_slice(grouped, w1_place(c), "w1_%d" % c))
 
-        def second_place(c):
-            return 2048 * (3 + c % 4)
+        def quantise_w3(c, grouped):
+            w3_q.append(quantise_weight_slice(grouped, w3_place(c), "w3_%d" % c))
 
         def gather(window, offsets, dtype, name):
             picked = keep.tile([P, S], dtype, name=name, align_bytes=64)
-            nc.vector.tensor_copy(picked[:], window.bitcast(dtype).indirect(offsets[:]))
+            nc.vector.tensor_copy(picked[:], window[:].bitcast(dtype).indirect(offsets[:]))
             return picked
 
         def product(acc, lhs, lhs_scale, rhs, rhs_scale):
             for a in range(PASSES):
                 nc.tensor.matmul_mx(
-                    out=acc[:], lhsT=lhs[a], lhsT_scale=lhs_scale[a], rhs=rhs[a], rhs_scale=rhs_scale[a],
+                    out=acc, lhsT=lhs[a], lhsT_scale=lhs_scale[a], rhs=rhs[a], rhs_scale=rhs_scale[a],
                     start=(a == 0), stop=(a == PASSES - 1),
                 )
-            return acc
 
-        def chip_weight(entry):
-            codes, scales, c0 = entry
-            return (
-                [codes[:, a, c0 : c0 + P].bitcast(E4M3) for a in range(PASSES)],
-                [scales[:, a, c0 : c0 + P] for a in range(PASSES)],
-            )
-
-        h1_bank, x_bank = banks[0], banks[1]
-        amp_banks, angle_banks = (banks[5], banks[2]), (banks[6], banks[7])
-        z_banks, back_banks = banks[0:2], banks[3:5]
-        out_banks = [banks[5], banks[6], banks[7], banks[2], banks[3], banks[4], banks[0], banks[1]]
-        tail_banks = back_banks + z_banks
-        starts = [sum(CHUNKS[:i]) for i in range(len(CHUNKS))]
-
-        table = keep.tile([P, 1], F32, name="table")
-        nc.vector.memset(table[:], 0.0)
-        nc.scalar.activation(table[:], table[:], ACT.Silu)
-
-        v_plane = zeroed_plane([P, T], "v_plane", nc.gpsimd)
-        v2_plane = zeroed_plane([P, T], "v2_plane")
-        v2_second = zeroed_plane([P, S], "v2_second")
-        idx = load_list(offs, "idx")
-        v_words = [load_words(tab_words[0].rearrange("p t i -> p (t i)"), T, "v_words0")]
-        load_table_scales(v_plane, tab_scales)
-        w1_raw = [load_weight_chunk(w1, starts[0], CHUNKS[0])]
-        v_words.append(load_words(tab_words[1].rearrange("p t i -> p (t i)"), T, "v_words1"))
-        idx2 = load_list(offs2, "idx2")
-        load_table_scales(v2_plane, tab2_scales)
-        idx3 = load_list(offs3, "idx3")
-        wg1_sb = keep.tile([P, S], F32, name="wg1_sb")
-        nc.sync.dma_start(wg1_sb[:], wg1)
-        idx4 = load_list(offs4, "idx4")
-        gain_rows = keep.tile([P, P], F32, name="gain_rows")
-        nc.gpsimd.memset(gain_rows[:], 0.0)
-        nc.sync.dma_start(gain_rows[0:SLICES, :], gain.rearrange("(c p) -> c p", p=P))
-        v2_words = [load_words(tab2_words[0].rearrange("p t i -> p (t i)"), T, "v2_words0")]
-        w3_raw = [load_weight_chunk(w3, starts[0], CHUNKS[0])]
-        w1_raw.append(load_weight_chunk(w1, starts[1], CHUNKS[1]))
-        v2_words.append(load_words(tab2_words[1].rearrange("p t i -> p (t i)"), T, "v2_words1"))
-        w2_plane = zeroed_plane([P, PASSES, H], "w2_plane")
-        w2_sb = keep.tile([P, PASSES, 2 * H], U8, name="w2_sb", align_bytes=64)
-        nc.sync.dma_start(w2_sb[:].bitcast(I32), w2_words.bitcast(I32).rearrange("a p c -> p a c"))
-        load_weight_scales(w2_plane, w2_scales)
-        wg2_sb = keep.tile([P, S], F32, name="wg2_sb")
-        nc.sync.dma_start(wg2_sb[:], wg2)
-        w1_raw.append(load_weight_chunk(w1, starts[2], CHUNKS[2]))
-        w3_raw.append(load_weight_chunk(w3, starts[1], CHUNKS[1]))
-
-        def load_dig(c):
-            rows = ring.tile([P, T2], F32, name="dig_rows", tag="dig", bufs=4)
-            nc.sync.dma_start(rows[:], dig[c * P : (c + 1) * P, :])
-            return rows
-
-        dig_sb = [load_dig(0)]
-        w1_raw.append(load_weight_chunk(w1, starts[3], CHUNKS[3]))
-        w3_raw.append(load_weight_chunk(w3, starts[2], CHUNKS[2]))
-        dig_sb.append(load_dig(1))
-        w3_raw.append(load_weight_chunk(w3, starts[3], CHUNKS[3]))
-        dig_sb.extend(load_dig(c) for c in (2, 3))
-        w4_plane = zeroed_plane([P, PASSES, N], "w4_plane")
-        w4_sb = [load_words(w4_words[a].rearrange("p n i -> p (n i)"), N, "w4_sb%d" % a) for a in range(PASSES)]
-        load_weight_scales(w4_plane, w4_scales)
-
-        pages_a = [keep.tile([P, T2], F32, name="page_a%d" % c) for c in range(4)]
-        pages_b = [keep.tile([P, T2], F32, name="page_b%d" % c) for c in range(1)]
-        for page in pages_a[:3]:
-            nc.gpsimd.memset(page[:], 0.0)
-        for page in pages_a[3:] + pages_b:
-            nc.vector.memset(page[:], 0.0)
-        ident = keep.tile([P, P], F32, name="ident")
-        make_identity(nc, ident[:])
-
-        v_codes = [gather(v_words[0][:], idx, U32, "v_codes0")]
-        v_scales = gather(v_plane[:], idx, U8, "v_scales")
-        v_codes.append(gather(v_words[1][:], idx, U32, "v_codes1"))
-        v_rhs = [v_codes[a][:].bitcast(E4M3) for a in range(PASSES)]
-        v_rhs_scale = [v_scales[4 * a :, :] for a in range(PASSES)]
-
-        w1_q, w3_q = [], []
-
-        def quantise_w1(c, grouped):
-            w1_q.append(quantise_weight_slice(grouped, first_place(c), "w1_%d" % c))
-
-        def quantise_w3(c, grouped):
-            w3_q.append(quantise_weight_slice(grouped, second_place(c), "w3_%d" % c))
+        def add_transposed(bank, src, blocks, start, stop):
+            for i in range(blocks):
+                nc.tensor.matmul(
+                    bank[:, i * P : (i + 1) * P], src[:, i * P : (i + 1) * P], ident[:],
+                    start=(start and i == 0), stop=(stop and i == blocks - 1), is_transpose=True,
+                )
 
         def place_first(c):
-            product(h1_bank, *chip_weight(w1_q[c]), v_rhs, v_rhs_scale)
-            th = ring.tile([P, S], F32, name="th", tag="th")
-            nc.scalar.activation(th[:], h1_bank[:], ACT.Tanh)
-            nc.vector.tensor_tensor(pages_a[c % 4][:].indirect(idx3[:]), th[:], wg1_sb[:], ALU.mult)
-
-        quantise_w1(0, round_weight_slice(w1_raw, 0))
-        quantise_w1(1, round_weight_slice(w1_raw, 1))
-        place_first(0)
-        v2_scales = gather(v2_plane[:], idx2, U8, "v2_scales")
-        for q in range(4):
-            nc.gpsimd.dma_start(
-                v2_second[:].bitcast(I32)[32 * q : 32 * q + 4, :],
-                v2_scales[:].bitcast(I32)[32 * q + 4 : 32 * q + 8, :],
+            codes, scales = w1_q[c]
+            product(
+                h1_bank[:],
+                [codes[:, a, :].bitcast(E4M3) for a in range(PASSES)],
+                [scales[:, a, :] for a in range(PASSES)],
+                [v_codes[a][:].bitcast(E4M3) for a in range(PASSES)],
+                [v_scales[4 * a :, :] for a in range(PASSES)],
             )
+            bent = ring.tile([P, S], F32, name="bent", tag="bent")
+            nc.scalar.activation(bent[:], h1_bank[:], ACT.Tanh)
+            nc.vector.tensor_tensor(first_pages[c % FIRST_PAGES][:].indirect(idx3[:]), bent[:], wg1_sb[:], ALU.mult)
 
-        v2_codes = [gather(v2_words[a][:], idx2, U32, "v2_codes%d" % a) for a in range(PASSES)]
-        v2_rhs = [v2_codes[a][:].bitcast(E4M3) for a in range(PASSES)]
-        v2_rhs_scale = [v2_scales[:], v2_second[:]]
-
-        def reduce_angle(c):
-            codes, scales, c0 = w3_q[c]
+        def count_turns(c):
+            codes, scales = w3_q[c]
             for j0 in range(0, S, P):
-                for a in range(PASSES):
-                    nc.tensor.matmul_mx(
-                        out=x_bank[:, j0 : j0 + P],
-                        lhsT=v2_codes[a][:, j0 : j0 + P].bitcast(E4M3), lhsT_scale=v2_scales[4 * a :, j0 : j0 + P],
-                        rhs=codes[:, a, :].bitcast(E4M3), rhs_scale=scales[:, a, :],
-                        start=(a == 0), stop=(a == PASSES - 1),
-                    )
+                product(
+                    x_bank[:, j0 : j0 + P],
+                    [v2_codes[a][:, j0 : j0 + P].bitcast(E4M3) for a in range(PASSES)],
+                    [v2_scales[4 * a :, j0 : j0 + P] for a in range(PASSES)],
+                    [codes[:, a, :].bitcast(E4M3) for a in range(PASSES)],
+                    [scales[:, a, :] for a in range(PASSES)],
+                )
             y = ring.tile([P, S], F32, name="y", tag="y")
             nc.scalar.activation(y[:], x_bank[:], ACT.Abs, bias=-math.pi / 2)
-            turns = ring.tile([P, S], U32, name="turns", tag="turns")
-            nc.scalar.activation(turns[:], y[:], ACT.Copy, scale=1 / (2 * math.pi))
-            back = ring.tile([P, S], F32, name="back", tag="back")
-            nc.scalar.activation(back[:], turns[:], ACT.Copy, scale=-2 * math.pi)
-            return y, back
+            periods = ring.tile([P, S], U32, name="periods", tag="periods")
+            nc.scalar.activation(periods[:], y[:], ACT.Copy, scale=1 / (2 * math.pi))
+            taken_off = ring.tile([P, S], F32, name="taken_off", tag="taken_off")
+            nc.scalar.activation(taken_off[:], periods[:], ACT.Copy, scale=-2 * math.pi)
+            return y, taken_off
 
-        def wave(c, y, back):
-            angle_bank = angle_banks[c % 2]
-            for k, term in enumerate((y, back)):
-                for j0 in range(0, S, P):
-                    nc.tensor.matmul(
-                        angle_bank[:, j0 : j0 + P], term[:, j0 : j0 + P], ident[:],
-                        start=(k == 0 and j0 == 0), stop=(k == 1 and j0 == S - P), is_transpose=True,
-                    )
-            angle = cycle.tile([P, S], F32, name="angle%d" % c, offset=first_place(c + 5))
-            nc.scalar.activation(angle[:], angle_bank[:], ACT.Abs)
-            nc.scalar.activation(angle[:], angle[:], ACT.Sin, scale=-1.0, bias=math.pi / 2)
-            return angle
+        def make_wave(c, y, taken_off):
+            rest = angle_banks[c % 2]
+            add_transposed(rest, y, S // P, True, False)
+            add_transposed(rest, taken_off, S // P, False, True)
+            wave = shared.tile([P, S], F32, name="wave%d" % c, offset=w1_place(c + LEAD_W1))
+            nc.scalar.activation(wave[:], rest[:], ACT.Abs)
+            nc.scalar.activation(wave[:], wave[:], ACT.Sin, scale=-1.0, bias=math.pi / 2)
+            return wave
 
-        def place_second(c, angle):
+        def place_second(c, wave):
             amp_bank = amp_banks[c % 2]
             product(
-                amp_bank,
+                amp_bank[:],
                 [w2_sb[:, a, 2 * P * c : 2 * P * (c + 1)].bitcast(E2M1) for a in range(PASSES)],
-                [w2_plane[:, a, P * c : P * (c + 1)] for a in range(PASSES)],
-                v2_rhs, v2_rhs_scale,
+                [w2_scale_sb[:, a, P * c : P * (c + 1)] for a in range(PASSES)],
+                [v2_codes[a][:].bitcast(E4M3) for a in range(PASSES)],
+                [v2_scales[:], v2_scales_pass1[:]],
             )
-            amp = cycle.tile([P, S], F32, name="amp%d" % c, offset=second_place(c))
+            amp = shared.tile([P, S], F32, name="amp%d" % c, offset=w3_place(c))
             nc.vector.tensor_tensor(amp[:], amp_bank[:], wg2_sb[:], ALU.mult)
-            page_b = pages_b[0]
-            nc.vector.tensor_tensor(page_b[:].indirect(idx4[:]), angle[:], amp[:], ALU.mult)
+            nc.vector.tensor_tensor(second_page[:].indirect(idx4[:]), wave[:], amp[:], ALU.mult)
+            width = QUARTER if c == SLICES - 1 else BANK
             parts = []
-            width = QUARTER if c == SLICES - 1 else HALF
             for m0 in range(0, T2, width):
                 cols = slice(m0, m0 + width)
-                larger = ring.tile([P, width], F32, name="larger", tag="larger", bufs=4)
+                larger = ring.tile([P, width], F32, name="larger", tag="larger", bufs=OUT_BUFS)
                 nc.vector.scalar_tensor_tensor(
-                    larger[:], pages_a[c % 4][:, cols], gain_sb[:, c : c + 1], page_b[:, cols], ALU.mult, ALU.max
+                    larger[:], first_pages[c % FIRST_PAGES][:, cols], gain_sb[:, c : c + 1], second_page[:, cols],
+                    ALU.mult, ALU.max,
                 )
                 parts.append(larger)
             return parts
 
-        def turn_dig(c, part, blocks, bank):
-            m0 = part * blocks * P
-            for i in range(blocks):
-                nc.tensor.matmul(
-                    bank[:, i * P : (i + 1) * P], dig_sb[c][:, m0 + i * P : m0 + (i + 1) * P],
-                    ident[:], start=(i == 0), stop=False, is_transpose=True,
-                )
+        def open_z(c, part, width, bank):
+            add_transposed(bank, dig_sb[c][:, part * width : (part + 1) * width], width // P, True, False)
 
-        def add_larger(c, part, larger, bank, copy):
+        def close_z(c, part, larger, bank, copy):
             blocks = larger.shape[1] // P
-            for i in range(blocks):
-                nc.tensor.matmul(
-                    bank[:, i * P : (i + 1) * P], larger[:, i * P : (i + 1) * P],
-                    ident[:], start=False, stop=(i == blocks - 1), is_transpose=True,
-                )
-            q0 = 32 * (c % 4)
-            h, i0 = divmod(part * blocks, 4)
+            add_transposed(bank, larger, blocks, False, True)
+            q0 = (P // PACK) * (c % SLICES_A_PASS)
+            half, i0 = divmod(part * blocks, BANK // P)
             copy(
-                z_t[c // 4][h][:, i0 : i0 + blocks, :, q0 : q0 + 32, :],
+                z_t[c // SLICES_A_PASS][half][:, i0 : i0 + blocks, :, q0 : q0 + P // PACK, :],
                 bank[:, 0 : blocks * P].rearrange("p (i q u e) -> p i u q e", i=blocks, u=2, e=2),
             )
 
-        def turn_back(z_half, g, back, copy):
-            words = z_half[:].rearrange("p i u q e -> p (i u q e)").bitcast(F32)
-            for i in range(4):
-                col = (4 * g + i) * P
-                nc.tensor.transpose(back[:, i * P : (i + 1) * P], words[:, col : col + P], ident[:])
-            grouped = ring.tile([P, QUARTER, PACK], BF16, name="z_grouped", tag="w_grouped", bufs=5, align_bytes=64)
+        def turn_back(a, quarter, bank, copy):
+            half, g = divmod(quarter, 2)
+            words = z_t[a][half][:].rearrange("p i u q e -> p (i u q e)").bitcast(F32)
+            for i in range(BANK // P):
+                col = g * BANK + i * P
+                nc.tensor.transpose(bank[:, i * P : (i + 1) * P], words[:, col : col + P], ident[:])
+            grouped = ring.tile([P, QUARTER, PACK], BF16, name="z_grouped", tag="grouped", bufs=GROUPED_BUFS, align_bytes=64)
             copy(
-                grouped[:].rearrange("p m j -> p (m j)").bitcast(F32).rearrange("p (i m u) -> p i m u", i=2, u=2),
-                back[:].rearrange("p (i u m) -> p i m u", i=2, u=2),
+                grouped[:].rearrange("p m t -> p (m t)").bitcast(F32).rearrange("p (i m u) -> p i m u", i=2, u=2),
+                bank[:].rearrange("p (i u m) -> p i m u", i=2, u=2),
             )
             return grouped
 
-        def quantise_z(grouped, name, place):
-            if place is None:
-                codes = keep.tile([P, QUARTER], U32, name=name + "_codes", align_bytes=64)
-            else:
-                codes = cycle.tile([P, QUARTER], U32, name=name + "_codes", align_bytes=64, offset=place)
-            scales = keep.tile([P, QUARTER], U8, name=name + "_scales", align_bytes=64)
-            nc.vector.quantize_mx(out=codes[:].bitcast(E4M3), scales=scales[:], in_=grouped[:].rearrange("p m j -> p (m j)"))
-            return codes, scales
-
-        place_first(1)
-        quantise_w3(0, round_weight_slice(w3_raw, 0))
-        quantise_w3(1, round_weight_slice(w3_raw, 1))
-        quantise_w1(2, round_weight_slice(w1_raw, 2))
-        quantise_w1(3, round_weight_slice(w1_raw, 3))
-        place_first(2)
-        staged = [reduce_angle(0), reduce_angle(1)]
-        angles = [wave(0, *staged[0])]
-        nc.tensor.transpose(banks[3][:, 0:P], gain_rows[:], ident[:])
-        gain_sb = keep.tile([P, SLICES], F32, name="gain_sb")
-        nc.scalar.copy(gain_sb[:], banks[3][:, 0:SLICES])
-        quantise_w1(4, round_weight_slice(w1_raw, 4))
-        quantise_w3(2, round_weight_slice(w3_raw, 2))
-        quantise_w3(3, round_weight_slice(w3_raw, 3))
-
-        z_q = [[], []]
-        z_t = [[keep.tile([P, 4, 2, P, 2], BF16, name="z_t%d_%d" % (b, h)) for h in range(2)] for b in range(PASSES)]
-        placed = []
-        for c in range(SLICES):
-            if c + 3 < SLICES:
-                place_first(c + 3)
-            if c + 2 < SLICES:
-                staged.append(reduce_angle(c + 2))
-            if c + 1 < SLICES:
-                angles.append(wave(c + 1, *staged[c + 1]))
-            if c >= 1:
-                for h in range(2):
-                    turn_dig(c - 1, h, 4, z_banks[h])
-                    add_larger(c - 1, h, placed[c - 1][h], z_banks[h], nc.scalar.copy)
-                if c + 3 < SLICES:
-                    dig_sb.append(load_dig(c + 3))
-            if c + 5 < SLICES:
-                w1_next = round_weight_slice(w1_raw, c + 5)
-            if c + 4 < SLICES:
-                w3_next = round_weight_slice(w3_raw, c + 4)
-            placed.append(place_second(c, angles[c]))
-            if c + 5 < SLICES:
-                quantise_w1(c + 5, w1_next)
-            if c + 4 < SLICES:
-                quantise_w3(c + 4, w3_next)
-            if c in (4, 5):
-                for g in range(2):
-                    grouped = turn_back(z_t[0][c - 4], g, back_banks[g], nc.scalar.copy)
-                    z_q[0].append(quantise_z(grouped, "z0_%d_%d" % (c - 4, g), second_place(c) + 1024 * g))
+        def quantise_z(a, quarter, grouped, codes):
+            scales = keep.tile([P, QUARTER], U8, name="z%d_%d_scales" % (a, quarter), align_bytes=64)
+            nc.vector.quantize_mx(out=codes[:].bitcast(E4M3), scales=scales[:], in_=grouped[:].rearrange("p m t -> p (m t)"))
+            z_q[a].append((codes, scales))
 
         def score_pass(a, quarter, pair):
             acc = out_banks[2 * quarter + pair]
@@ -373,29 +256,143 @@ def tile_list_buried_wall_score_kernel(
                 n0 = (2 * pair + j) * P
                 nc.tensor.matmul_mx(
                     out=acc[:, j * QUARTER : (j + 1) * QUARTER],
-                    lhsT=w4_sb[a][:, n0 : n0 + P].bitcast(E4M3), lhsT_scale=w4_plane[:, a, n0 : n0 + P],
+                    lhsT=w4_sb[a][:, n0 : n0 + P].bitcast(E4M3), lhsT_scale=w4_scale_sb[:, a, n0 : n0 + P],
                     rhs=codes[:].bitcast(E4M3), rhs_scale=scales[:],
                     start=(a == 0 and j == 0), stop=(a == PASSES - 1 and j == 1),
                 )
 
+        table_warm_up = keep.tile([P, 1], F32, name="table_warm_up")
+        nc.vector.memset(table_warm_up[:], 0.0)
+        nc.scalar.activation(table_warm_up[:], table_warm_up[:], ACT.Silu)
+
+        v_scale_sb = zeroed_scales([P, T], "v_scale_sb", nc.gpsimd)
+        v2_scale_sb = zeroed_scales([P, T], "v2_scale_sb", nc.vector)
+        v2_scales_pass1 = zeroed_scales([P, S], "v2_scales_pass1", nc.vector)
+        idx = load_list(offs, "idx")
+        v_words = [load_words(tab_words[0], "v_words0")]
+        load_table_scales(v_scale_sb, tab_scales)
+        w1_raw = [load_weight_chunk(w1, 0)]
+        v_words.append(load_words(tab_words[1], "v_words1"))
+        idx2 = load_list(offs2, "idx2")
+        load_table_scales(v2_scale_sb, tab2_scales)
+        idx3 = load_list(offs3, "idx3")
+        wg1_sb = load_rows(wg1, "wg1_sb")
+        idx4 = load_list(offs4, "idx4")
+        gain_rows = keep.tile([P, P], F32, name="gain_rows")
+        nc.gpsimd.memset(gain_rows[:], 0.0)
+        nc.sync.dma_start(gain_rows[0:SLICES, :], gain.rearrange("(c p) -> c p", p=P))
+        v2_words = [load_words(tab2_words[0], "v2_words0")]
+        w3_raw = [load_weight_chunk(w3, 0)]
+        w1_raw.append(load_weight_chunk(w1, 1))
+        v2_words.append(load_words(tab2_words[1], "v2_words1"))
+        w2_scale_sb = zeroed_scales([P, PASSES, H], "w2_scale_sb", nc.vector)
+        w2_sb = keep.tile([P, PASSES, 2 * H], U8, name="w2_sb", align_bytes=64)
+        nc.sync.dma_start(w2_sb[:].bitcast(I32), w2_words.bitcast(I32).rearrange("a p c -> p a c"))
+        load_weight_scales(w2_scale_sb, w2_scales)
+        wg2_sb = load_rows(wg2, "wg2_sb")
+        dig_sb = []
+        for i in range(1, H // CHUNK):
+            if i + 1 < H // CHUNK:
+                w1_raw.append(load_weight_chunk(w1, i + 1))
+            w3_raw.append(load_weight_chunk(w3, i))
+            dig_sb.append(load_dig(i - 1))
+        dig_sb.append(load_dig(DIG_BUFS - 1))
+        w4_scale_sb = zeroed_scales([P, PASSES, N], "w4_scale_sb", nc.vector)
+        w4_sb = [load_words(w4_words[a], "w4_sb%d" % a) for a in range(PASSES)]
+        load_weight_scales(w4_scale_sb, w4_scales)
+
+        first_pages = [keep.tile([P, T2], F32, name="first_page%d" % c) for c in range(FIRST_PAGES)]
+        second_page = keep.tile([P, T2], F32, name="second_page")
+        for page in first_pages[:-1]:
+            nc.gpsimd.memset(page[:], 0.0)
+        for page in (first_pages[-1], second_page):
+            nc.vector.memset(page[:], 0.0)
+        ident = keep.tile([P, P], F32, name="ident")
+        make_identity(nc, ident[:])
+
+        w1_q, w3_q = [], []
+        v_codes = [gather(v_words[0], idx, U32, "v_codes0")]
+        v_scales = gather(v_scale_sb, idx, U8, "v_scales")
+        v_codes.append(gather(v_words[1], idx, U32, "v_codes1"))
+        quantise_w1(0, round_weight_slice(w1_raw, 0))
+        quantise_w1(1, round_weight_slice(w1_raw, 1))
+        place_first(0)
+        v2_scales = gather(v2_scale_sb, idx2, U8, "v2_scales")
+        for q in range(QUADRANTS):
+            nc.gpsimd.dma_start(
+                v2_scales_pass1[:].bitcast(I32)[32 * q : 32 * q + 4, :],
+                v2_scales[:].bitcast(I32)[32 * q + 4 : 32 * q + 8, :],
+            )
+        v2_codes = [gather(v2_words[a], idx2, U32, "v2_codes%d" % a) for a in range(PASSES)]
+        place_first(1)
+        for c in (0, 1):
+            quantise_w3(c, round_weight_slice(w3_raw, c))
+        for c in (2, 3):
+            quantise_w1(c, round_weight_slice(w1_raw, c))
+        place_first(2)
+        turns = [count_turns(c) for c in range(LEAD_TURNS)]
+        waves = [make_wave(0, *turns[0])]
+        nc.tensor.transpose(back_banks[0][:, 0:P], gain_rows[:], ident[:])
+        gain_sb = keep.tile([P, SLICES], F32, name="gain_sb")
+        nc.scalar.copy(gain_sb[:], back_banks[0][:, 0:SLICES])
+        quantise_w1(4, round_weight_slice(w1_raw, 4))
+        for c in (2, 3):
+            quantise_w3(c, round_weight_slice(w3_raw, c))
+
+        z_q = [[], []]
+        z_t = [[keep.tile([P, BANK // P, 2, P, 2], BF16, name="z_t%d_%d" % (a, half)) for half in range(2)] for a in range(PASSES)]
+        maxima = []
+        for c in range(SLICES):
+            if c + LEAD_FIRST_PAGE < SLICES:
+                place_first(c + LEAD_FIRST_PAGE)
+            if c + LEAD_TURNS < SLICES:
+                turns.append(count_turns(c + LEAD_TURNS))
+            if c + LEAD_WAVE < SLICES:
+                waves.append(make_wave(c + LEAD_WAVE, *turns[c + LEAD_WAVE]))
+            if c >= 1:
+                for half in range(2):
+                    open_z(c - 1, half, BANK, z_banks[half])
+                    close_z(c - 1, half, maxima[c - 1][half], z_banks[half], nc.scalar.copy)
+                if c - 1 + DIG_BUFS < SLICES:
+                    dig_sb.append(load_dig(c - 1 + DIG_BUFS))
+            if c + LEAD_W1 < SLICES:
+                w1_next = round_weight_slice(w1_raw, c + LEAD_W1)
+            if c + LEAD_W3 < SLICES:
+                w3_next = round_weight_slice(w3_raw, c + LEAD_W3)
+            maxima.append(place_second(c, waves[c]))
+            if c + LEAD_W1 < SLICES:
+                quantise_w1(c + LEAD_W1, w1_next)
+            if c + LEAD_W3 < SLICES:
+                quantise_w3(c + LEAD_W3, w3_next)
+            half = c - SLICES_A_PASS
+            if half in (0, 1):
+                for g in range(2):
+                    quarter = 2 * half + g
+                    grouped = turn_back(0, quarter, back_banks[g], nc.scalar.copy)
+                    codes = shared.tile(
+                        [P, QUARTER], U32, name="z0_%d_codes" % quarter, align_bytes=64, offset=w3_place(c) + g * PLACE // 2
+                    )
+                    quantise_z(0, quarter, grouped, codes)
+
+        last = SLICES - 1
+        tail_copies = (nc.scalar.copy, nc.vector.tensor_copy)
         for quarter in range(2):
             for pair in range(2):
                 score_pass(0, quarter, pair)
         for quarter in range(4):
-            turn_dig(SLICES - 1, quarter, 2, tail_banks[quarter])
+            open_z(last, quarter, QUARTER, tail_banks[quarter])
         for quarter in range(4):
-            add_larger(SLICES - 1, quarter, placed[-1][quarter], tail_banks[quarter], (nc.scalar.copy, nc.vector.tensor_copy)[quarter // 2])
+            close_z(last, quarter, maxima[last][quarter], tail_banks[quarter], tail_copies[quarter // 2])
         for quarter in range(4):
-            h, g = divmod(quarter, 2)
-            grouped = turn_back(z_t[1][h], g, tail_banks[quarter], (nc.scalar.copy, nc.vector.tensor_copy)[h])
-            z_q[1].append(quantise_z(grouped, "z1_%d" % quarter, None))
+            grouped = turn_back(1, quarter, tail_banks[quarter], tail_copies[quarter // 2])
+            codes = keep.tile([P, QUARTER], U32, name="z1_%d_codes" % quarter, align_bytes=64)
+            quantise_z(1, quarter, grouped, codes)
         for quarter in range(4):
             for pair in range(2):
-                acc = out_banks[2 * quarter + pair]
                 if quarter >= 2:
                     score_pass(0, quarter, pair)
                 score_pass(1, quarter, pair)
-                score = ring.tile([P, HALF], F32, name="score", tag=("score", "larger")[quarter // 2], bufs=4)
-                nc.scalar.activation(score[:], acc[:], ACT.Abs)
+                score = ring.tile([P, BANK], F32, name="score", tag=("score", "larger")[quarter // 2], bufs=OUT_BUFS)
+                nc.scalar.activation(score[:], out_banks[2 * quarter + pair][:], ACT.Abs)
                 rows = out[2 * pair * P : 2 * (pair + 1) * P, quarter * QUARTER : (quarter + 1) * QUARTER]
                 nc.sync.dma_start(rows.rearrange("(j p) m -> p j m", p=P), score[:].rearrange("p (j m) -> p j m", j=2))

@@ -34,7 +34,7 @@ LEAD_W1, LEAD_FIRST_PAGE = 5, 3
 LEAD_W3, LEAD_TURNS, LEAD_WAVE = 4, 2, 1
 FIRST_PAGES = LEAD_FIRST_PAGE + 1
 W1_PLACES, W3_PLACES = 3, 4
-RAW_BUFS = 12
+RAW_BUFS = 10
 GROUPED_BUFS = 5
 DIG_BUFS = 4
 OUT_BUFS = 4
@@ -63,6 +63,9 @@ def tile_list_buried_wall_score_kernel(
 
         def w3_place(c):
             return PLACE * (W1_PLACES + c % W3_PLACES)
+
+        def late_page_place(a):
+            return PLACE * (W1_PLACES + W3_PLACES + 2 * a)
 
         def load_list(src, name):
             tile = keep.tile([P, S // 16], U16, name=name)
@@ -98,14 +101,15 @@ def tile_list_buried_wall_score_kernel(
                     src[:, 4 * q : 4 * q + 4, :].bitcast(I32).rearrange("a r c -> r a c"),
                 )
 
-        def load_weight_chunk(w, i):
-            raws = []
+        def load_weight_rows(w, i, raws):
             for a in range(PASSES):
-                raw = ring.tile([P, PACK, CHUNK], F32, name="raw", tag="raw", bufs=RAW_BUFS)
                 rows = w[a * K_PASS : (a + 1) * K_PASS, i * CHUNK : (i + 1) * CHUNK]
-                nc.sync.dma_start(raw[:], rows.rearrange("(p t) c -> p t c", t=PACK))
-                raws.append(raw)
+                nc.sync.dma_start(raws[a][:], rows.rearrange("(p t) c -> p t c", t=PACK))
             return raws
+
+        def load_weight_chunk(w, i):
+            raws = [ring.tile([P, PACK, CHUNK], F32, name="raw", tag="raw", bufs=RAW_BUFS) for a in range(PASSES)]
+            return load_weight_rows(w, i, raws)
 
         def load_dig(c):
             rows = ring.tile([P, T2], F32, name="dig_rows", tag="dig", bufs=DIG_BUFS)
@@ -206,7 +210,7 @@ def tile_list_buried_wall_score_kernel(
             amp = shared.tile([P, S], F32, name="amp%d" % c, offset=w3_place(c))
             nc.vector.tensor_tensor(amp[:], amp_bank[:], wg2_sb[:], ALU.mult)
             nc.vector.tensor_tensor(second_page[:].indirect(idx4[:]), wave[:], amp[:], ALU.mult)
-            width = QUARTER if c == SLICES - 1 else BANK
+            width = QUARTER if c == SLICES - 1 else T2
             parts = []
             for m0 in range(0, T2, width):
                 cols = slice(m0, m0 + width)
@@ -282,7 +286,8 @@ def tile_list_buried_wall_score_kernel(
         nc.gpsimd.memset(gain_rows[:], 0.0)
         nc.sync.dma_start(gain_rows[0:SLICES, :], gain.rearrange("(c p) -> c p", p=P))
         v2_words = [load_words(tab2_words[0], "v2_words0")]
-        w3_raw = [load_weight_chunk(w3, 0)]
+        w3_first = [shared.tile([P, PACK, CHUNK], F32, name="w3_first%d" % a, offset=late_page_place(a)) for a in range(PASSES)]
+        w3_raw = [load_weight_rows(w3, 0, w3_first)]
         w1_raw.append(load_weight_chunk(w1, 1))
         v2_words.append(load_words(tab2_words[1], "v2_words1"))
         w2_scale_sb = zeroed_scales([P, PASSES, H], "w2_scale_sb", nc.vector)
@@ -301,11 +306,9 @@ def tile_list_buried_wall_score_kernel(
         w4_sb = [load_words(w4_words[a], "w4_sb%d" % a) for a in range(PASSES)]
         load_weight_scales(w4_scale_sb, w4_scales)
 
-        first_pages = [keep.tile([P, T2], F32, name="first_page%d" % c) for c in range(FIRST_PAGES)]
+        first_pages = [keep.tile([P, T2], F32, name="first_page%d" % c) for c in range(FIRST_PAGES - PASSES)]
         second_page = keep.tile([P, T2], F32, name="second_page")
-        for page in first_pages[:-1]:
-            nc.gpsimd.memset(page[:], 0.0)
-        for page in (first_pages[-1], second_page):
+        for page in first_pages + [second_page]:
             nc.vector.memset(page[:], 0.0)
         ident = keep.tile([P, P], F32, name="ident")
         make_identity(nc, ident[:])
@@ -327,6 +330,10 @@ def tile_list_buried_wall_score_kernel(
         place_first(1)
         for c in (0, 1):
             quantise_w3(c, round_weight_slice(w3_raw, c))
+        for a in range(PASSES):
+            page = shared.tile([P, T2], F32, name="late_page%d" % a, offset=late_page_place(a))
+            nc.gpsimd.memset(page[:], 0.0)
+            first_pages.append(page)
         for c in (2, 3):
             quantise_w1(c, round_weight_slice(w1_raw, c))
         place_first(2)
@@ -352,7 +359,7 @@ def tile_list_buried_wall_score_kernel(
             if c >= 1:
                 for half in range(2):
                     open_z(c - 1, half, BANK, z_banks[half])
-                    close_z(c - 1, half, maxima[c - 1][half], z_banks[half], nc.scalar.copy)
+                    close_z(c - 1, half, maxima[c - 1][0][:, half * BANK : (half + 1) * BANK], z_banks[half], nc.scalar.copy)
                 if c - 1 + DIG_BUFS < SLICES:
                     dig_sb.append(load_dig(c - 1 + DIG_BUFS))
             if c + LEAD_W1 < SLICES:

import math
from contextlib import ExitStack

import concourse.mybir as mybir
from concourse.masks import make_identity

K, T, S, H, T2, N = 1024, 2048, 512, 1024, 1024, 512
FLOPS = 2 * (3 * K * H * S + H * N * T2)

F32 = mybir.dt.float32
BF16 = mybir.dt.bfloat16
I32 = mybir.dt.int32
U32 = mybir.dt.uint32
U16 = mybir.dt.uint16
U8 = mybir.dt.uint8
E4M3 = mybir.dt.float8_e4m3fn_x4
E2M1 = mybir.dt.float4_e2m1fn_x4
ACT = mybir.ActivationFunctionType
ALU = mybir.AluOpType

P = 128
PACK = 4
K_PASS = P * PACK
PASSES = 2
QUADRANTS = 4
SLICES = H // P
SLICES_A_PASS = K_PASS // P
BANK = 512
QUARTER = 256
CHUNK = 256
PLACE = 2048

LEAD_W1, LEAD_FIRST_PAGE = 5, 3
LEAD_W3, LEAD_TURNS, LEAD_WAVE = 4, 2, 1
FIRST_PAGES = LEAD_FIRST_PAGE + 1
W1_PLACES, W3_PLACES = 3, 4
RAW_BUFS = 10
GROUPED_BUFS = 5
DIG_BUFS = 4
OUT_BUFS = 4


def tile_list_buried_wall_score_kernel(
    tc, tab_words, tab_scales, tab2_words, tab2_scales, offs, offs2, offs3, offs4,
    w1, gain, w2_words, w2_scales, w3, wg1, wg2, dig, w4_words, w4_scales, out,
):
    nc = tc.nc
    with ExitStack() as ctx:
        keep = ctx.enter_context(tc.tile_pool(name="keep", bufs=1))
        ring = ctx.enter_context(tc.tile_pool(name="ring", bufs=2))
        shared = ctx.enter_context(tc.tile_pool(name="shared", bufs=1))
        psum = ctx.enter_context(tc.psum_pool(name="psum", bufs=1))
        banks = [psum.tile([P, BANK], F32, name="bank%d" % b) for b in range(8)]

        h1_bank, x_bank = banks[0], banks[1]
        z_banks, back_banks = banks[0:2], banks[3:5]
        amp_banks, angle_banks = (banks[5], banks[2]), (banks[6], banks[7])
        tail_banks = back_banks + z_banks
        out_banks = [banks[5], banks[6], banks[7], banks[2]] + tail_banks

        def w1_place(c):
            return PLACE * (c % W1_PLACES)

        def w3_place(c):
            return PLACE * (W1_PLACES + c % W3_PLACES)

        def late_page_place(a):
            return PLACE * (W1_PLACES + W3_PLACES + 2 * a)

        def load_list(src, name):
            tile = keep.tile([P, S // 16], U16, name=name)
            nc.sync.dma_start(tile[:], src)
            return tile

        def load_words(src, name):
            tile = keep.tile([P, src.shape[1]], I32, name=name, align_bytes=64)
            nc.sync.dma_start(tile[:], src.rearrange("p c t -> p (c t)").bitcast(I32))
            return tile

        def load_rows(src, name):
            tile = keep.tile([P, S], F32, name=name)
            nc.sync.dma_start(tile[:], src)
            return tile

        def zeroed_scales(shape, name, engine):
            tile = keep.tile(shape, U8, name=name, align_bytes=64)
            engine.memset(tile[:].bitcast(I32), 0)
            return tile

        def load_table_scales(tile, src):
            for q in range(QUADRANTS):
                nc.sync.dma_start(
                    tile[:].bitcast(I32)[32 * q : 32 * q + 8, :],
                    src[:, 4 * q : 4 * q + 4, :].bitcast(I32),
                )

        def load_weight_scales(tile, src):
            for q in range(QUADRANTS):
                nc.sync.dma_start(
                    tile[:].bitcast(I32)[32 * q : 32 * q + 4, :, :],
                    src[:, 4 * q : 4 * q + 4, :].bitcast(I32).rearrange("a r c -> r a c"),
                )

        def load_weight_rows(w, i, raws):
            for a in range(PASSES):
                rows = w[a * K_PASS : (a + 1) * K_PASS, i * CHUNK : (i + 1) * CHUNK]
                nc.sync.dma_start(raws[a][:], rows.rearrange("(p t) c -> p t c", t=PACK))
            return raws

        def load_weight_chunk(w, i):
            raws = [ring.tile([P, PACK, CHUNK], F32, name="raw", tag="raw", bufs=RAW_BUFS) for a in range(PASSES)]
            return load_weight_rows(w, i, raws)

        def load_dig(c):
            rows = ring.tile([P, T2], F32, name="dig_rows", tag="dig", bufs=DIG_BUFS)
            nc.sync.dma_start(rows[:], dig[c * P : (c + 1) * P, :])
            return rows

        def round_weight_slice(chunks, c):
            i, c0 = divmod(c * P, CHUNK)
            grouped = ring.tile([P, PASSES, P, PACK], BF16, name="w_grouped", tag="grouped", bufs=GROUPED_BUFS, align_bytes=64)
            for a in range(PASSES):
                nc.scalar.copy(grouped[:, a], chunks[i][a][:, :, c0 : c0 + P].rearrange("p t c -> p c t"))
            return grouped

        def quantise_weight_slice(grouped, place, name):
            codes = shared.tile([P, PASSES, P], U32, name=name + "_codes", align_bytes=64, offset=place)
            scales = shared.tile([P, PASSES, P], U8, name=name + "_scales", align_bytes=64, offset=place + PLACE // 2)
            nc.vector.quantize_mx(
                out=codes[:].rearrange("p a c -> p (a c)").bitcast(E4M3),
                scales=scales[:].rearrange("p a c -> p (a c)"),
                in_=grouped[:].rearrange("p a c t -> p (a c t)"),
            )
            return codes, scales

        def quantise_w1(c, grouped):
            w1_q.append(quantise_weight_slice(grouped, w1_place(c), "w1_%d" % c))

        def quantise_w3(c, grouped):
            w3_q.append(quantise_weight_slice(grouped, w3_place(c), "w3_%d" % c))

        def gather(window, offsets, dtype, name):
            picked = keep.tile([P, S], dtype, name=name, align_bytes=64)
            nc.vector.tensor_copy(picked[:], window[:].bitcast(dtype).indirect(offsets[:]))
            return picked

        def product(acc, lhs, lhs_scale, rhs, rhs_scale):
            for a in range(PASSES):
                nc.tensor.matmul_mx(
                    out=acc, lhsT=lhs[a], lhsT_scale=lhs_scale[a], rhs=rhs[a], rhs_scale=rhs_scale[a],
                    start=(a == 0), stop=(a == PASSES - 1),
                )

        def add_transposed(bank, src, blocks, start, stop):
            for i in range(blocks):
                nc.tensor.matmul(
                    bank[:, i * P : (i + 1) * P], src[:, i * P : (i + 1) * P], ident[:],
                    start=(start and i == 0), stop=(stop and i == blocks - 1), is_transpose=True,
                )

        def place_first(c):
            codes, scales = w1_q[c]
            product(
                h1_bank[:],
                [codes[:, a, :].bitcast(E4M3) for a in range(PASSES)],
                [scales[:, a, :] for a in range(PASSES)],
                [v_codes[a][:].bitcast(E4M3) for a in range(PASSES)],
                [v_scales[4 * a :, :] for a in range(PASSES)],
            )
            bent = ring.tile([P, S], F32, name="bent", tag="bent")
            nc.scalar.activation(bent[:], h1_bank[:], ACT.Tanh)
            nc.vector.tensor_tensor(first_pages[c % FIRST_PAGES][:].indirect(idx3[:]), bent[:], wg1_sb[:], ALU.mult)

        def count_turns(c):
            codes, scales = w3_q[c]
            for j0 in range(0, S, P):
                product(
                    x_bank[:, j0 : j0 + P],
                    [v2_codes[a][:, j0 : j0 + P].bitcast(E4M3) for a in range(PASSES)],
                    [v2_scales[4 * a :, j0 : j0 + P] for a in range(PASSES)],
                    [codes[:, a, :].bitcast(E4M3) for a in range(PASSES)],
                    [scales[:, a, :] for a in range(PASSES)],
                )
            y = ring.tile([P, S], F32, name="y", tag="y")
            nc.scalar.activation(y[:], x_bank[:], ACT.Abs, bias=-math.pi / 2)
            periods = ring.tile([P, S], U32, name="periods", tag="periods")
            nc.scalar.activation(periods[:], y[:], ACT.Copy, scale=1 / (2 * math.pi))
            taken_off = ring.tile([P, S], F32, name="taken_off", tag="taken_off")
            nc.scalar.activation(taken_off[:], periods[:], ACT.Copy, scale=-2 * math.pi)
            return y, taken_off

        def make_wave(c, y, taken_off):
            rest = angle_banks[c % 2]
            add_transposed(rest, y, S // P, True, False)
            add_transposed(rest, taken_off, S // P, False, True)
            wave = shared.tile([P, S], F32, name="wave%d" % c, offset=w1_place(c + LEAD_W1))
            nc.scalar.activation(wave[:], rest[:], ACT.Abs)
            nc.scalar.activation(wave[:], wave[:], ACT.Sin, scale=-1.0, bias=math.pi / 2)
            return wave

        def place_second(c, wave):
            amp_bank = amp_banks[c % 2]
            product(
                amp_bank[:],
                [w2_sb[:, a, 2 * P * c : 2 * P * (c + 1)].bitcast(E2M1) for a in range(PASSES)],
                [w2_scale_sb[:, a, P * c : P * (c + 1)] for a in range(PASSES)],
                [v2_codes[a][:].bitcast(E4M3) for a in range(PASSES)],
                [v2_scales[:], v2_scales_pass1[:]],
            )
            amp = shared.tile([P, S], F32, name="amp%d" % c, offset=w3_place(c))
            nc.vector.tensor_tensor(amp[:], amp_bank[:], wg2_sb[:], ALU.mult)
            nc.vector.tensor_tensor(second_page[:].indirect(idx4[:]), wave[:], amp[:], ALU.mult)
            width = QUARTER if c == SLICES - 1 else T2
            parts = []
            for m0 in range(0, T2, width):
                cols = slice(m0, m0 + width)
                larger = ring.tile([P, width], F32, name="larger", tag="larger", bufs=OUT_BUFS)
                nc.vector.scalar_tensor_tensor(
                    larger[:], first_pages[c % FIRST_PAGES][:, cols], gain_sb[:, c : c + 1], second_page[:, cols],
                    ALU.mult, ALU.max,
                )
                parts.append(larger)
            return parts

        def open_z(c, part, width, bank):
            add_transposed(bank, dig_sb[c][:, part * width : (part + 1) * width], width // P, True, False)

        def close_z(c, part, larger, bank, copy):
            blocks = larger.shape[1] // P
            add_transposed(bank, larger, blocks, False, True)
            q0 = (P // PACK) * (c % SLICES_A_PASS)
            half, i0 = divmod(part * blocks, BANK // P)
            copy(
                z_t[c // SLICES_A_PASS][half][:, i0 : i0 + blocks, :, q0 : q0 + P // PACK, :],
                bank[:, 0 : blocks * P].rearrange("p (i q u e) -> p i u q e", i=blocks, u=2, e=2),
            )

        def turn_back(a, quarter, bank, copy):
            half, g = divmod(quarter, 2)
            words = z_t[a][half][:].rearrange("p i u q e -> p (i u q e)").bitcast(F32)
            for i in range(BANK // P):
                col = g * BANK + i * P
                nc.tensor.transpose(bank[:, i * P : (i + 1) * P], words[:, col : col + P], ident[:])
            grouped = ring.tile([P, QUARTER, PACK], BF16, name="z_grouped", tag="grouped", bufs=GROUPED_BUFS, align_bytes=64)
            copy(
                grouped[:].rearrange("p m t -> p (m t)").bitcast(F32).rearrange("p (i m u) -> p i m u", i=2, u=2),
                bank[:].rearrange("p (i u m) -> p i m u", i=2, u=2),
            )
            return grouped

        def quantise_z(a, quarter, grouped, codes):
            scales = keep.tile([P, QUARTER], U8, name="z%d_%d_scales" % (a, quarter), align_bytes=64)
            nc.vector.quantize_mx(out=codes[:].bitcast(E4M3), scales=scales[:], in_=grouped[:].rearrange("p m t -> p (m t)"))
            z_q[a].append((codes, scales))

        def score_pass(a, quarter, pair):
            acc = out_banks[2 * quarter + pair]
            codes, scales = z_q[a][quarter]
            for j in range(2):
                n0 = (2 * pair + j) * P
                nc.tensor.matmul_mx(
                    out=acc[:, j * QUARTER : (j + 1) * QUARTER],
                    lhsT=w4_sb[a][:, n0 : n0 + P].bitcast(E4M3), lhsT_scale=w4_scale_sb[:, a, n0 : n0 + P],
                    rhs=codes[:].bitcast(E4M3), rhs_scale=scales[:],
                    start=(a == 0 and j == 0), stop=(a == PASSES - 1 and j == 1),
                )

        table_warm_up = keep.tile([P, 1], F32, name="table_warm_up")
        nc.vector.memset(table_warm_up[:], 0.0)
        nc.scalar.activation(table_warm_up[:], table_warm_up[:], ACT.Silu)

        v_scale_sb = zeroed_scales([P, T], "v_scale_sb", nc.gpsimd)
        v2_scale_sb = zeroed_scales([P, T], "v2_scale_sb", nc.vector)
        v2_scales_pass1 = zeroed_scales([P, S], "v2_scales_pass1", nc.vector)
        idx = load_list(offs, "idx")
        v_words = [load_words(tab_words[0], "v_words0")]
        load_table_scales(v_scale_sb, tab_scales)
        w1_raw = [load_weight_chunk(w1, 0)]
        v_words.append(load_words(tab_words[1], "v_words1"))
        idx2 = load_list(offs2, "idx2")
        load_table_scales(v2_scale_sb, tab2_scales)
        idx3 = load_list(offs3, "idx3")
        wg1_sb = load_rows(wg1, "wg1_sb")
        idx4 = load_list(offs4, "idx4")
        gain_rows = keep.tile([P, P], F32, name="gain_rows")
        nc.gpsimd.memset(gain_rows[:], 0.0)
        nc.sync.dma_start(gain_rows[0:SLICES, :], gain.rearrange("(c p) -> c p", p=P))
        v2_words = [load_words(tab2_words[0], "v2_words0")]
        w3_first = [shared.tile([P, PACK, CHUNK], F32, name="w3_first%d" % a, offset=late_page_place(a)) for a in range(PASSES)]
        w3_raw = [load_weight_rows(w3, 0, w3_first)]
        w1_raw.append(load_weight_chunk(w1, 1))
        v2_words.append(load_words(tab2_words[1], "v2_words1"))
        w2_scale_sb = zeroed_scales([P, PASSES, H], "w2_scale_sb", nc.vector)
        w2_sb = keep.tile([P, PASSES, 2 * H], U8, name="w2_sb", align_bytes=64)
        nc.sync.dma_start(w2_sb[:].bitcast(I32), w2_words.bitcast(I32).rearrange("a p c -> p a c"))
        load_weight_scales(w2_scale_sb, w2_scales)
        wg2_sb = load_rows(wg2, "wg2_sb")
        dig_sb = []
        for i in range(1, H // CHUNK):
            if i + 1 < H // CHUNK:
                w1_raw.append(load_weight_chunk(w1, i + 1))
            w3_raw.append(load_weight_chunk(w3, i))
            dig_sb.append(load_dig(i - 1))
        dig_sb.append(load_dig(DIG_BUFS - 1))
        w4_scale_sb = zeroed_scales([P, PASSES, N], "w4_scale_sb", nc.vector)
        w4_sb = [load_words(w4_words[a], "w4_sb%d" % a) for a in range(PASSES)]
        load_weight_scales(w4_scale_sb, w4_scales)

        first_pages = [keep.tile([P, T2], F32, name="first_page%d" % c) for c in range(FIRST_PAGES - PASSES)]
        second_page = keep.tile([P, T2], F32, name="second_page")
        for page in first_pages + [second_page]:
            nc.vector.memset(page[:], 0.0)
        ident = keep.tile([P, P], F32, name="ident")
        make_identity(nc, ident[:])

        w1_q, w3_q = [], []
        v_codes = [gather(v_words[0], idx, U32, "v_codes0")]
        v_scales = gather(v_scale_sb, idx, U8, "v_scales")
        v_codes.append(gather(v_words[1], idx, U32, "v_codes1"))
        quantise_w1(0, round_weight_slice(w1_raw, 0))
        quantise_w1(1, round_weight_slice(w1_raw, 1))
        place_first(0)
        v2_scales = gather(v2_scale_sb, idx2, U8, "v2_scales")
        for q in range(QUADRANTS):
            nc.gpsimd.dma_start(
                v2_scales_pass1[:].bitcast(I32)[32 * q : 32 * q + 4, :],
                v2_scales[:].bitcast(I32)[32 * q + 4 : 32 * q + 8, :],
            )
        v2_codes = [gather(v2_words[a], idx2, U32, "v2_codes%d" % a) for a in range(PASSES)]
        place_first(1)
        for c in (0, 1):
            quantise_w3(c, round_weight_slice(w3_raw, c))
        for a in range(PASSES):
            page = shared.tile([P, T2], F32, name="late_page%d" % a, offset=late_page_place(a))
            nc.gpsimd.memset(page[:], 0.0)
            first_pages.append(page)
        for c in (2, 3):
            quantise_w1(c, round_weight_slice(w1_raw, c))
        place_first(2)
        turns = [count_turns(c) for c in range(LEAD_TURNS)]
        waves = [make_wave(0, *turns[0])]
        nc.tensor.transpose(back_banks[0][:, 0:P], gain_rows[:], ident[:])
        gain_sb = keep.tile([P, SLICES], F32, name="gain_sb")
        nc.scalar.copy(gain_sb[:], back_banks[0][:, 0:SLICES])
        quantise_w1(4, round_weight_slice(w1_raw, 4))
        for c in (2, 3):
            quantise_w3(c, round_weight_slice(w3_raw, c))

        z_q = [[], []]
        z_t = [[keep.tile([P, BANK // P, 2, P, 2], BF16, name="z_t%d_%d" % (a, half)) for half in range(2)] for a in range(PASSES)]
        maxima = []
        for c in range(SLICES):
            if c + LEAD_FIRST_PAGE < SLICES:
                place_first(c + LEAD_FIRST_PAGE)
            if c + LEAD_TURNS < SLICES:
                turns.append(count_turns(c + LEAD_TURNS))
            if c + LEAD_WAVE < SLICES:
                waves.append(make_wave(c + LEAD_WAVE, *turns[c + LEAD_WAVE]))
            if c >= 1:
                for half in range(2):
                    open_z(c - 1, half, BANK, z_banks[half])
                    close_z(c - 1, half, maxima[c - 1][0][:, half * BANK : (half + 1) * BANK], z_banks[half], nc.scalar.copy)
                if c - 1 + DIG_BUFS < SLICES:
                    dig_sb.append(load_dig(c - 1 + DIG_BUFS))
            if c + LEAD_W1 < SLICES:
                w1_next = round_weight_slice(w1_raw, c + LEAD_W1)
            if c + LEAD_W3 < SLICES:
                w3_next = round_weight_slice(w3_raw, c + LEAD_W3)
            maxima.append(place_second(c, waves[c]))
            if c + LEAD_W1 < SLICES:
                quantise_w1(c + LEAD_W1, w1_next)
            if c + LEAD_W3 < SLICES:
                quantise_w3(c + LEAD_W3, w3_next)
            half = c - SLICES_A_PASS
            if half in (0, 1):
                for g in range(2):
                    quarter = 2 * half + g
                    grouped = turn_back(0, quarter, back_banks[g], nc.scalar.copy)
                    codes = shared.tile(
                        [P, QUARTER], U32, name="z0_%d_codes" % quarter, align_bytes=64, offset=w3_place(c) + g * PLACE // 2
                    )
                    quantise_z(0, quarter, grouped, codes)

        last = SLICES - 1
        tail_copies = (nc.scalar.copy, nc.vector.tensor_copy)
        for quarter in range(2):
            for pair in range(2):
                score_pass(0, quarter, pair)
        for quarter in range(4):
            open_z(last, quarter, QUARTER, tail_banks[quarter])
        for quarter in range(4):
            close_z(last, quarter, maxima[last][quarter], tail_banks[quarter], tail_copies[quarter // 2])
        for quarter in range(4):
            grouped = turn_back(1, quarter, tail_banks[quarter], tail_copies[quarter // 2])
            codes = keep.tile([P, QUARTER], U32, name="z1_%d_codes" % quarter, align_bytes=64)
            quantise_z(1, quarter, grouped, codes)
        for quarter in range(4):
            for pair in range(2):
                if quarter >= 2:
                    score_pass(0, quarter, pair)
                score_pass(1, quarter, pair)
                score = ring.tile([P, BANK], F32, name="score", tag=("score", "larger")[quarter // 2], bufs=OUT_BUFS)
                nc.scalar.activation(score[:], out_banks[2 * quarter + pair][:], ACT.Abs)
                rows = out[2 * pair * P : 2 * (pair + 1) * P, quarter * QUARTER : (quarter + 1) * QUARTER]
                nc.sync.dma_start(rows.rearrange("(j p) m -> p j m", p=P), score[:].rearrange("p (j m) -> p j m", j=2))
